import numpy as np
import ml_dtypes


def mxq(x, axis, fmt="e4m3"):
    dtype, down = {"e4m3": (ml_dtypes.float8_e4m3fn, 7), "e5m2": (ml_dtypes.float8_e5m2, 14)}[fmt]
    v = np.moveaxis(np.asarray(x, np.float32).astype(ml_dtypes.bfloat16).astype(np.float64), axis, -1)
    blocks = v.reshape(v.shape[:-1] + (-1, 32))
    amax = np.abs(blocks).max(-1, keepdims=True)
    byte = np.maximum(np.where(amax > 0, np.frexp(amax)[1] - 1 + 127, 0) - down, 1)
    scale = np.exp2(byte - 127.0)
    codes = (blocks / scale).astype(np.float32).astype(dtype).astype(np.float64)
    return np.moveaxis((codes * scale).reshape(v.shape), -1, axis)


WIDE = False


def mx_kscale(k):
    if not WIDE:
        return np.ones(k)
    levels = np.array([10, -10, 5, -5, 0])
    if k % 512:
        return np.exp2(np.random.permutation(np.resize(levels, k // 32))).repeat(32)
    a = np.empty((k // 512, 16))
    for p in range(k // 512):
        a[p, :8] = np.random.permutation(np.resize(levels, 8))
        for g in range(8):
            far = levels[np.abs(levels - a[p, g]) >= 10]
            a[p, g + 8] = far[np.random.randint(len(far))]
    return np.exp2(a.ravel()).repeat(32)


def f64(x):
    return np.asarray(x).astype(np.float64)


def striped(idx):
    return np.tile(idx.reshape(-1, 16).T, (8, 1)).astype(np.uint16)


def unstriped(offs):
    return offs[:16].T.reshape(-1).astype(np.int64)


E2M1 = np.array([0.0, 0.5, 1.0, 1.5, 2.0, 3.0, 4.0, 6.0, -0.0, -0.5, -1.0, -1.5, -2.0, -3.0, -4.0, -6.0])


def pack_weight(w, fmt):
    k, n = w.shape
    w = f64(np.asarray(w, np.float32).astype(ml_dtypes.bfloat16)).reshape(k // 32, 32, n)
    amax = np.abs(w).max(1)
    if fmt == "e4m3":
        byte = np.frexp(amax)[1] - 1 + 127 - 7
    else:
        mant, ex = np.frexp(amax / 6.0)
        byte = np.where(mant > 0.5, ex, ex - 1) + 127
    byte = np.clip(np.where(amax > 0, byte, 1), 1, 254)
    scaled = (w * np.exp2(127.0 - byte)[:, None, :]).reshape(k, n).astype(np.float32)
    by_word = np.ascontiguousarray(scaled.reshape(k // 512, 128, 4, n).transpose(0, 1, 3, 2))
    if fmt == "e4m3":
        words = by_word.astype(ml_dtypes.float8_e4m3fn).view(np.uint8)
    else:
        c = by_word.astype(ml_dtypes.float4_e2m1fn).view(np.uint8) & 0xF
        words = (c[..., 0::2] | (c[..., 1::2] << 4)).reshape(k // 512, 128, 2 * n)
    return np.ascontiguousarray(words), np.ascontiguousarray(byte.astype(np.uint8).reshape(k // 512, 16, n))


def unpack_weight(words, scales, fmt):
    g, _, n = scales.shape
    words = np.ascontiguousarray(words).reshape(g, 128, n, -1)
    if fmt == "e4m3":
        vals = words.view(ml_dtypes.float8_e4m3fn).astype(np.float64)
    else:
        nib = np.empty((g, 128, n, 4), np.uint8)
        nib[..., 0::2] = words & 0xF
        nib[..., 1::2] = words >> 4
        vals = E2M1[nib]
    vals = vals * np.repeat(np.exp2(scales.astype(np.float64) - 127.0), 8, axis=1)[..., None]
    return vals.transpose(0, 1, 3, 2).reshape(g * 512, n)


def sigmoid(v):
    return 1.0 / (1.0 + np.exp(-np.maximum(v, -700.0)))


K, T, E, C, H, N = 1024, 1024, 8, 256, 512, 128
R = 2


def by_expert(wq, xq):
    return np.concatenate([wq[e].T @ xq[:, e * C:(e + 1) * C] for e in range(E)], axis=1)


def setup_inputs():
    n = np.random.standard_normal
    s = mx_kscale(K)[:, None]
    u = mx_kscale(H)
    slot_token = np.concatenate([r * (T // R) + np.random.permutation(T // R)[:C // R] for e in range(E) for r in range(R)])
    x = pack_weight(n((K, T)) * s, "e4m3")
    return {
        "x_words": x[0],
        "x_scales": x[1],
        "w1": (n((E, K, H)) / np.sqrt(K) / s[None]).astype(np.float32),
        "w3": (n((E, K, H)) / np.sqrt(K) / s[None] * u[None, None, :]).astype(np.float32),
        "w2": (n((E, H, N)) / np.sqrt(H) / u[None, :, None]).astype(np.float32),
        "offs": striped(slot_token),
    }


def reference(x_words, x_scales, w1, w3, w2, offs):
    idx = unstriped(offs)
    xq = unpack_weight(x_words, x_scales, "e4m3")[:, idx]
    h = sigmoid(by_expert(mxq(f64(w1), 1, "e4m3"), xq))
    h = h * by_expert(mxq(f64(w3), 1, "e4m3"), xq)
    y = by_expert(mxq(f64(w2), 1, "e4m3"), mxq(h, 0, "e4m3"))
    return y.reshape(N, E, R, C // R).transpose(0, 2, 1, 3).reshape(N, E * C)

@@ -1,0 +1,178 @@
+from contextlib import ExitStack
+
+import concourse.mybir as mybir
+
+K, T, E, C, H, N = 1024, 1024, 8, 256, 512, 128
+R = 2
+FLOPS = 2 * E * C * (2 * K * H + H * N)
+
+F32 = mybir.dt.float32
+BF16 = mybir.dt.bfloat16
+I32 = mybir.dt.int32
+U32 = mybir.dt.uint32
+U16 = mybir.dt.uint16
+U8 = mybir.dt.uint8
+FP8X4 = mybir.dt.float8_e4m3fn_x4
+
+P = 128
+PACK = 4
+K_PASS = P * PACK
+PASSES = K // K_PASS
+U = C // R
+GATHER = 2 * C
+EARLY = 2
+
+
+def tile_moe_pke_glu_sigmoid_kernel(tc, x_words, x_scales, w1, w3, w2, offs, out):
+    nc = tc.nc
+    with ExitStack() as ctx:
+        keep = ctx.enter_context(tc.tile_pool(name="keep", bufs=1))
+        raw_pool = ctx.enter_context(tc.tile_pool(name="raw", bufs=10))
+        stage = ctx.enter_context(tc.tile_pool(name="stage", bufs=8))
+        code_pool = ctx.enter_context(tc.tile_pool(name="codes", bufs=12))
+        work = ctx.enter_context(tc.tile_pool(name="work", bufs=4))
+        psum_a = ctx.enter_context(tc.psum_pool(name="psum_a", bufs=3))
+        psum_y = ctx.enter_context(tc.psum_pool(name="psum_y", bufs=2))
+
+        offsets = keep.tile([P, E * C // 16], U16, name="offsets")
+        nc.sync.dma_start(offsets[:], offs)
+
+        token_scales = keep.tile([P, T // 4], I32, name="token_scales", align_bytes=64)
+        nc.vector.memset(token_scales[:], 0)
+        for q in range(4):
+            nc.sync.dma_start(
+                token_scales[32 * q : 32 * q + 4 * PASSES, :],
+                x_scales[:, 4 * q : 4 * q + 4, :].bitcast(I32),
+            )
+        token_words = []
+        for o in range(PASSES):
+            words = keep.tile([P, T], I32, name="token_words%d" % o, align_bytes=64)
+            nc.sync.dma_start(words[:], x_words[o].rearrange("p t r -> p (t r)").bitcast(I32))
+            token_words.append(words)
+
+        result = keep.tile([P, R, E, U], F32, name="result")
+        out_view = out.rearrange("n (m e u) -> n m e u", m=R, e=E)
+
+        def gather(g):
+            entries = offsets[:, g * GATHER // 16 : (g + 1) * GATHER // 16]
+            slot_words = []
+            for o in range(PASSES):
+                words = keep.tile([P, GATHER], U32, name="slot_words%d_%d" % (g, o), align_bytes=64)
+                nc.vector.tensor_copy(words[:], token_words[o][:].bitcast(U32).indirect(entries))
+                slot_words.append(words)
+            slot_scales = keep.tile([P, GATHER], U8, name="slot_scales%d" % g, align_bytes=64)
+            nc.vector.tensor_copy(slot_scales[:], token_scales[:].bitcast(U8).indirect(entries))
+            return slot_words, slot_scales
+
+        def first_layer_codes(w, e, o, on_vector, split):
+            raw = raw_pool.tile([P, PACK, H], F32, name="raw", tag="raw")
+            nc.sync.dma_start(raw[:], w[e, o * K_PASS : (o + 1) * K_PASS, :].rearrange("(p j) c -> p j c", j=PACK))
+            grouped = stage.tile([P, PACK * H], BF16, name="grouped", align_bytes=64)
+            src = raw[:].rearrange("p j (m t) -> p m j t", t=PACK)
+            dst = grouped[:].rearrange("p (t m j) -> p m j t", t=PACK, j=PACK)
+            if on_vector:
+                nc.vector.tensor_copy(dst, src)
+            else:
+                nc.scalar.copy(dst, src)
+            codes = code_pool.tile([P, H], U32, name="codes", align_bytes=64)
+            scales = code_pool.tile([P, H], U8, name="scales", align_bytes=64)
+            width = H // split
+            for s in range(split):
+                cols = slice(s * width, (s + 1) * width)
+                nc.vector.quantize_mx(
+                    out=codes[:, cols].bitcast(FP8X4),
+                    scales=scales[:, cols],
+                    in_=grouped[:, PACK * s * width : PACK * (s + 1) * width],
+                )
+            return codes, scales
+
+        def first_layer_product(weights, slots, first, tag):
+            slot_words, slot_scales = slots
+            bank = psum_a.tile([P, PACK, U], F32, name=tag, tag=tag)
+            cols = slice(first, first + U)
+            for t in range(PACK):
+                for o in range(PASSES):
+                    codes, scales = weights[o]
+                    nc.tensor.matmul_mx(
+                        out=bank[:, t, :],
+                        lhsT=codes[:, t * P : (t + 1) * P].bitcast(FP8X4),
+                        lhsT_scale=scales[:, t * P : (t + 1) * P],
+                        rhs=slot_words[o][:, cols].bitcast(FP8X4),
+                        rhs_scale=slot_scales[4 * o :, cols],
+                        start=(o == 0),
+                        stop=(o == PASSES - 1),
+                    )
+            return bank
+
+        def hidden_codes(e, slots):
+            last = e == E - 1
+            w1_codes = [first_layer_codes(w1, e, o, o == 0 and e % 2 == 1, 1) for o in range(PASSES)]
+            w3_codes = [first_layer_codes(w3, e, 0, False, 1)]
+            w3_codes.append(first_layer_codes(w3, e, 1, True, PACK if last else 1))
+            gates = []
+            for m in range(R):
+                bank = first_layer_product(w1_codes, slots, (e * C) % GATHER + m * U, "a1")
+                gate = work.tile([P, U, PACK], F32, name="gate")
+                nc.scalar.activation(gate[:], bank[:].rearrange("p t u -> p u t"), mybir.ActivationFunctionType.Sigmoid)
+                gates.append(gate)
+            hidden = work.tile([P, C, PACK], BF16, name="hidden", align_bytes=64)
+            for m in range(R):
+                bank = first_layer_product(w3_codes, slots, (e * C) % GATHER + m * U, "a3")
+                nc.vector.tensor_tensor(
+                    hidden[:, m * U : (m + 1) * U, :], bank[:].rearrange("p t u -> p u t"), gates[m][:], mybir.AluOpType.mult
+                )
+            codes = keep.tile([P, C], U32, name="hidden_codes%d" % e, align_bytes=64)
+            scales = keep.tile([P, C], U8, name="hidden_scales%d" % e, align_bytes=64)
+            nc.vector.quantize_mx(out=codes[:].bitcast(FP8X4), scales=scales[:], in_=hidden[:].rearrange("p c t -> p (c t)"))
+            return codes, scales
+
+        def second_layer_codes(e0, count):
+            raw = raw_pool.tile([P, count, PACK, N], F32, name="raw", tag="raw")
+            nc.sync.dma_start(raw[:], w2[e0 : e0 + count].rearrange("e (p j) n -> p e j n", j=PACK))
+            grouped = stage.tile([P, count, N * PACK], BF16, name="grouped", align_bytes=64)
+            for d in range(count):
+                nc.scalar.copy(
+                    grouped[:, d, :].rearrange("p (c i j) -> p c j i", i=4, j=PACK),
+                    raw[:, d, :, :].rearrange("p j (c i) -> p c j i", i=4),
+                )
+            codes = code_pool.tile([P, count * N], U32, name="codes", align_bytes=64)
+            scales = code_pool.tile([P, count * N], U8, name="scales", align_bytes=64)
+            nc.vector.quantize_mx(out=codes[:].bitcast(FP8X4), scales=scales[:], in_=grouped[:].rearrange("p d x -> p (d x)"))
+            return codes, scales
+
+        def second_layer_product(weights, d, e0, count, hidden):
+            codes, scales = weights
+            bank = psum_y.tile([P, count, R, U], F32, name="y", tag="y")
+            for i in range(count):
+                h_codes, h_scales = hidden[e0 + i]
+                cols = slice((d + i) * N, (d + i + 1) * N)
+                nc.tensor.matmul_mx(
+                    out=bank[:, i, :, :].rearrange("p m u -> p (m u)"),
+                    lhsT=codes[:, cols].bitcast(FP8X4),
+                    lhsT_scale=scales[:, cols],
+                    rhs=h_codes[:].bitcast(FP8X4),
+                    rhs_scale=h_scales[:],
+                    start=True,
+                    stop=True,
+                )
+            nc.scalar.copy(result[:, :, e0 : e0 + count, :].rearrange("p m e u -> p e m u"), bank[:])
+
+        hidden = []
+        slots = None
+        for e in range(E):
+            if (e * C) % GATHER == 0:
+                slots = gather(e * C // GATHER)
+            hidden.append(hidden_codes(e, slots))
+            if e == EARLY - 1:
+                weights = second_layer_codes(0, EARLY)
+                second_layer_product(weights, 0, 0, EARLY, hidden)
+        for e0 in range(EARLY, E - 2, 2):
+            weights = second_layer_codes(e0, 2)
+            second_layer_product(weights, 0, e0, 2, hidden)
+        nc.sync.dma_start(out_view[:, :, 0:4, :], result[:, :, 0:4, :])
+        nc.sync.dma_start(out_view[:, :, 4:6, :], result[:, :, 4:6, :])
+        weights = second_layer_codes(E - 2, 2)
+        for d in range(2):
+            e = E - 2 + d
+            second_layer_product(weights, d, e, 1, hidden)
+            nc.sync.dma_start(out_view[:, :, e, :], result[:, :, e, :])

@@ -19,8 +19,7 @@ PACK = 4
 K_PASS = P * PACK
 PASSES = K // K_PASS
 U = C // R
-GATHER = 2 * C
-EARLY = 2
+GATHER = C
 
 
 def tile_moe_pke_glu_sigmoid_kernel(tc, x_words, x_scales, w1, w3, w2, offs, out):
@@ -30,6 +29,7 @@ def tile_moe_pke_glu_sigmoid_kernel(tc, x_words, x_scales, w1, w3, w2, offs, out
         raw_pool = ctx.enter_context(tc.tile_pool(name="raw", bufs=10))
         stage = ctx.enter_context(tc.tile_pool(name="stage", bufs=8))
         code_pool = ctx.enter_context(tc.tile_pool(name="codes", bufs=12))
+        slot_pool = ctx.enter_context(tc.tile_pool(name="slots", bufs=3))
         work = ctx.enter_context(tc.tile_pool(name="work", bufs=4))
         psum_a = ctx.enter_context(tc.psum_pool(name="psum_a", bufs=3))
         psum_y = ctx.enter_context(tc.psum_pool(name="psum_y", bufs=2))
@@ -50,30 +50,29 @@ def tile_moe_pke_glu_sigmoid_kernel(tc, x_words, x_scales, w1, w3, w2, offs, out
             nc.sync.dma_start(words[:], x_words[o].rearrange("p t r -> p (t r)").bitcast(I32))
             token_words.append(words)
 
-        result = keep.tile([P, R, E, U], F32, name="result")
         out_view = out.rearrange("n (m e u) -> n m e u", m=R, e=E)
 
         def gather(g):
             entries = offsets[:, g * GATHER // 16 : (g + 1) * GATHER // 16]
             slot_words = []
             for o in range(PASSES):
-                words = keep.tile([P, GATHER], U32, name="slot_words%d_%d" % (g, o), align_bytes=64)
+                words = slot_pool.tile([P, GATHER], U32, name="slot_words%d" % o, align_bytes=64)
                 nc.vector.tensor_copy(words[:], token_words[o][:].bitcast(U32).indirect(entries))
                 slot_words.append(words)
-            slot_scales = keep.tile([P, GATHER], U8, name="slot_scales%d" % g, align_bytes=64)
+            slot_scales = slot_pool.tile([P, GATHER], U8, name="slot_scales", align_bytes=64)
             nc.vector.tensor_copy(slot_scales[:], token_scales[:].bitcast(U8).indirect(entries))
             return slot_words, slot_scales
 
-        def first_layer_codes(w, e, o, on_vector, split):
+        def first_layer_codes(w, e, o, vector_tiles, split):
             raw = raw_pool.tile([P, PACK, H], F32, name="raw", tag="raw")
             nc.sync.dma_start(raw[:], w[e, o * K_PASS : (o + 1) * K_PASS, :].rearrange("(p j) c -> p j c", j=PACK))
             grouped = stage.tile([P, PACK * H], BF16, name="grouped", align_bytes=64)
             src = raw[:].rearrange("p j (m t) -> p m j t", t=PACK)
             dst = grouped[:].rearrange("p (t m j) -> p m j t", t=PACK, j=PACK)
-            if on_vector:
-                nc.vector.tensor_copy(dst, src)
-            else:
-                nc.scalar.copy(dst, src)
+            if vector_tiles > 0:
+                nc.vector.tensor_copy(dst[:, :, :, :vector_tiles], src[:, :, :, :vector_tiles])
+            if vector_tiles < PACK:
+                nc.scalar.copy(dst[:, :, :, vector_tiles:], src[:, :, :, vector_tiles:])
             codes = code_pool.tile([P, H], U32, name="codes", align_bytes=64)
             scales = code_pool.tile([P, H], U8, name="scales", align_bytes=64)
             width = H // split
@@ -106,9 +105,10 @@ def tile_moe_pke_glu_sigmoid_kernel(tc, x_words, x_scales, w1, w3, w2, offs, out
 
         def hidden_codes(e, slots):
             last = e == E - 1
-            w1_codes = [first_layer_codes(w1, e, o, o == 0 and e % 2 == 1, 1) for o in range(PASSES)]
-            w3_codes = [first_layer_codes(w3, e, 0, False, 1)]
-            w3_codes.append(first_layer_codes(w3, e, 1, True, PACK if last else 1))
+            w1_codes = [first_layer_codes(w1, e, 0, PACK, 1)]
+            w3_codes = [first_layer_codes(w3, e, 0, 0, 1)]
+            w1_codes.append(first_layer_codes(w1, e, 1, PACK // 2, 1))
+            w3_codes.append(first_layer_codes(w3, e, 1, PACK // 2 if last else 0, PACK if last else 1))
             gates = []
             for m in range(R):
                 bank = first_layer_product(w1_codes, slots, (e * C) % GATHER + m * U, "a1")
@@ -131,7 +131,8 @@ def tile_moe_pke_glu_sigmoid_kernel(tc, x_words, x_scales, w1, w3, w2, offs, out
             nc.sync.dma_start(raw[:], w2[e0 : e0 + count].rearrange("e (p j) n -> p e j n", j=PACK))
             grouped = stage.tile([P, count, N * PACK], BF16, name="grouped", align_bytes=64)
             for d in range(count):
-                nc.scalar.copy(
+                copy = nc.vector.tensor_copy if d == 1 and e0 > 0 else nc.scalar.copy
+                copy(
                     grouped[:, d, :].rearrange("p (c i j) -> p c j i", i=4, j=PACK),
                     raw[:, d, :, :].rearrange("p j (c i) -> p c j i", i=4),
                 )
@@ -155,7 +156,9 @@ def tile_moe_pke_glu_sigmoid_kernel(tc, x_words, x_scales, w1, w3, w2, offs, out
                     start=True,
                     stop=True,
                 )
-            nc.scalar.copy(result[:, :, e0 : e0 + count, :].rearrange("p m e u -> p e m u"), bank[:])
+            result = keep.tile([P, R, count, U], F32, name="result%d" % e0)
+            nc.scalar.copy(result[:].rearrange("p m e u -> p e m u"), bank[:])
+            nc.sync.dma_start(out_view[:, :, e0 : e0 + count, :], result[:])
 
         hidden = []
         slots = None
@@ -163,16 +166,6 @@ def tile_moe_pke_glu_sigmoid_kernel(tc, x_words, x_scales, w1, w3, w2, offs, out
             if (e * C) % GATHER == 0:
                 slots = gather(e * C // GATHER)
             hidden.append(hidden_codes(e, slots))
-            if e == EARLY - 1:
-                weights = second_layer_codes(0, EARLY)
-                second_layer_product(weights, 0, 0, EARLY, hidden)
-        for e0 in range(EARLY, E - 2, 2):
+        for e0 in range(0, E, 2):
             weights = second_layer_codes(e0, 2)
             second_layer_product(weights, 0, e0, 2, hidden)
-        nc.sync.dma_start(out_view[:, :, 0:4, :], result[:, :, 0:4, :])
-        nc.sync.dma_start(out_view[:, :, 4:6, :], result[:, :, 4:6, :])
-        weights = second_layer_codes(E - 2, 2)
-        for d in range(2):
-            e = E - 2 + d
-            second_layer_product(weights, d, e, 1, hidden)
-            nc.sync.dma_start(out_view[:, :, e, :], result[:, :, e, :])

@@ -19,7 +19,7 @@ PACK = 4
 K_PASS = P * PACK
 PASSES = K // K_PASS
 U = C // R
-GATHER = C
+GATHER = 2 * C
 
 
 def tile_moe_pke_glu_sigmoid_kernel(tc, x_words, x_scales, w1, w3, w2, offs, out):
@@ -27,13 +27,19 @@ def tile_moe_pke_glu_sigmoid_kernel(tc, x_words, x_scales, w1, w3, w2, offs, out
     with ExitStack() as ctx:
         keep = ctx.enter_context(tc.tile_pool(name="keep", bufs=1))
         raw_pool = ctx.enter_context(tc.tile_pool(name="raw", bufs=10))
-        stage = ctx.enter_context(tc.tile_pool(name="stage", bufs=8))
-        code_pool = ctx.enter_context(tc.tile_pool(name="codes", bufs=12))
-        slot_pool = ctx.enter_context(tc.tile_pool(name="slots", bufs=3))
+        stage = ctx.enter_context(tc.tile_pool(name="stage", bufs=10))
+        code_pool = ctx.enter_context(tc.tile_pool(name="codes", bufs=14))
+        slot_pool = ctx.enter_context(tc.tile_pool(name="slots", bufs=2))
         work = ctx.enter_context(tc.tile_pool(name="work", bufs=4))
         psum_a = ctx.enter_context(tc.psum_pool(name="psum_a", bufs=3))
         psum_y = ctx.enter_context(tc.psum_pool(name="psum_y", bufs=2))
 
+        def load_pass(w, e, o):
+            raw = raw_pool.tile([P, PACK, H], F32, name="raw", tag="raw")
+            nc.sync.dma_start(raw[:], w[e, o * K_PASS : (o + 1) * K_PASS, :].rearrange("(p j) c -> p j c", j=PACK))
+            return raw
+
+        first_raw = load_pass(w1, 0, 0)
         offsets = keep.tile([P, E * C // 16], U16, name="offsets")
         nc.sync.dma_start(offsets[:], offs)
 
@@ -52,6 +58,10 @@ def tile_moe_pke_glu_sigmoid_kernel(tc, x_words, x_scales, w1, w3, w2, offs, out
 
         out_view = out.rearrange("n (m e u) -> n m e u", m=R, e=E)
 
+        on_vector = [nc.vector.tensor_copy]
+        on_scalar = [nc.scalar.copy]
+        on_both = on_vector + on_scalar
+
         def gather(g):
             entries = offsets[:, g * GATHER // 16 : (g + 1) * GATHER // 16]
             slot_words = []
@@ -63,27 +73,23 @@ def tile_moe_pke_glu_sigmoid_kernel(tc, x_words, x_scales, w1, w3, w2, offs, out
             nc.vector.tensor_copy(slot_scales[:], token_scales[:].bitcast(U8).indirect(entries))
             return slot_words, slot_scales
 
-        def first_layer_codes(w, e, o, vector_tiles, split):
-            raw = raw_pool.tile([P, PACK, H], F32, name="raw", tag="raw")
-            nc.sync.dma_start(raw[:], w[e, o * K_PASS : (o + 1) * K_PASS, :].rearrange("(p j) c -> p j c", j=PACK))
-            grouped = stage.tile([P, PACK * H], BF16, name="grouped", align_bytes=64)
+        def first_layer_codes(raw, copies):
             src = raw[:].rearrange("p j (m t) -> p m j t", t=PACK)
-            dst = grouped[:].rearrange("p (t m j) -> p m j t", t=PACK, j=PACK)
-            if vector_tiles > 0:
-                nc.vector.tensor_copy(dst[:, :, :, :vector_tiles], src[:, :, :, :vector_tiles])
-            if vector_tiles < PACK:
-                nc.scalar.copy(dst[:, :, :, vector_tiles:], src[:, :, :, vector_tiles:])
-            codes = code_pool.tile([P, H], U32, name="codes", align_bytes=64)
-            scales = code_pool.tile([P, H], U8, name="scales", align_bytes=64)
-            width = H // split
-            for s in range(split):
-                cols = slice(s * width, (s + 1) * width)
-                nc.vector.quantize_mx(
-                    out=codes[:, cols].bitcast(FP8X4),
-                    scales=scales[:, cols],
-                    in_=grouped[:, PACK * s * width : PACK * (s + 1) * width],
-                )
-            return codes, scales
+            tiles = PACK // len(copies)
+            parts = []
+            for i, copy in enumerate(copies):
+                grouped = stage.tile([P, tiles * P * PACK], BF16, name="grouped", align_bytes=64)
+                copy(grouped[:].rearrange("p (t m j) -> p m j t", t=tiles, j=PACK), src[:, :, :, i * tiles : (i + 1) * tiles])
+                parts.append(grouped)
+            stationary = []
+            for grouped in parts:
+                codes = code_pool.tile([P, tiles * P], U32, name="codes", align_bytes=64)
+                scales = code_pool.tile([P, tiles * P], U8, name="scales", align_bytes=64)
+                nc.vector.quantize_mx(out=codes[:].bitcast(FP8X4), scales=scales[:], in_=grouped[:])
+                for t in range(tiles):
+                    cols = slice(t * P, (t + 1) * P)
+                    stationary.append((codes[:, cols].bitcast(FP8X4), scales[:, cols]))
+            return stationary
 
         def first_layer_product(weights, slots, first, tag):
             slot_words, slot_scales = slots
@@ -91,11 +97,11 @@ def tile_moe_pke_glu_sigmoid_kernel(tc, x_words, x_scales, w1, w3, w2, offs, out
             cols = slice(first, first + U)
             for t in range(PACK):
                 for o in range(PASSES):
-                    codes, scales = weights[o]
+                    codes, scales = weights[o][t]
                     nc.tensor.matmul_mx(
                         out=bank[:, t, :],
-                        lhsT=codes[:, t * P : (t + 1) * P].bitcast(FP8X4),
-                        lhsT_scale=scales[:, t * P : (t + 1) * P],
+                        lhsT=codes,
+                        lhsT_scale=scales,
                         rhs=slot_words[o][:, cols].bitcast(FP8X4),
                         rhs_scale=slot_scales[4 * o :, cols],
                         start=(o == 0),
@@ -105,10 +111,10 @@ def tile_moe_pke_glu_sigmoid_kernel(tc, x_words, x_scales, w1, w3, w2, offs, out
 
         def hidden_codes(e, slots):
             last = e == E - 1
-            w1_codes = [first_layer_codes(w1, e, 0, PACK, 1)]
-            w3_codes = [first_layer_codes(w3, e, 0, 0, 1)]
-            w1_codes.append(first_layer_codes(w1, e, 1, PACK // 2, 1))
-            w3_codes.append(first_layer_codes(w3, e, 1, PACK // 2 if last else 0, PACK if last else 1))
+            w1_codes = [first_layer_codes(first_raw if e == 0 else load_pass(w1, e, 0), on_vector)]
+            w3_codes = [first_layer_codes(load_pass(w3, e, 0), on_scalar)]
+            w1_codes.append(first_layer_codes(load_pass(w1, e, 1), on_both))
+            w3_codes.append(first_layer_codes(load_pass(w3, e, 1), on_both if last else on_scalar))
             gates = []
             for m in range(R):
                 bank = first_layer_product(w1_codes, slots, (e * C) % GATHER + m * U, "a1")
@@ -129,16 +135,17 @@ def tile_moe_pke_glu_sigmoid_kernel(tc, x_words, x_scales, w1, w3, w2, offs, out
         def second_layer_codes(e0, count):
             raw = raw_pool.tile([P, count, PACK, N], F32, name="raw", tag="raw")
             nc.sync.dma_start(raw[:], w2[e0 : e0 + count].rearrange("e (p j) n -> p e j n", j=PACK))
-            grouped = stage.tile([P, count, N * PACK], BF16, name="grouped", align_bytes=64)
-            for d in range(count):
-                copy = nc.vector.tensor_copy if d == 1 and e0 > 0 else nc.scalar.copy
-                copy(
-                    grouped[:, d, :].rearrange("p (c i j) -> p c j i", i=4, j=PACK),
-                    raw[:, d, :, :].rearrange("p j (c i) -> p c j i", i=4),
-                )
             codes = code_pool.tile([P, count * N], U32, name="codes", align_bytes=64)
             scales = code_pool.tile([P, count * N], U8, name="scales", align_bytes=64)
-            nc.vector.quantize_mx(out=codes[:].bitcast(FP8X4), scales=scales[:], in_=grouped[:].rearrange("p d x -> p (d x)"))
+            for d in range(count):
+                copy = nc.vector.tensor_copy if d == 1 else nc.scalar.copy
+                grouped = stage.tile([P, N * PACK], BF16, name="grouped", align_bytes=64)
+                copy(
+                    grouped[:].rearrange("p (c i j) -> p c j i", i=4, j=PACK),
+                    raw[:, d, :, :].rearrange("p j (c i) -> p c j i", i=4),
+                )
+                cols = slice(d * N, (d + 1) * N)
+                nc.vector.quantize_mx(out=codes[:, cols].bitcast(FP8X4), scales=scales[:, cols], in_=grouped[:])
             return codes, scales
 
         def second_layer_product(weights, d, e0, count, hidden):

@@ -46,15 +46,12 @@ def tile_moe_pke_glu_sigmoid_kernel(tc, x_words, x_scales, w1, w3, w2, offs, out
         token_scales = keep.tile([P, T // 4], I32, name="token_scales", align_bytes=64)
         nc.vector.memset(token_scales[:], 0)
         for q in range(4):
-            nc.sync.dma_start(
+            nc.gpsimd.dma_start(
                 token_scales[32 * q : 32 * q + 4 * PASSES, :],
                 x_scales[:, 4 * q : 4 * q + 4, :].bitcast(I32),
             )
-        token_words = []
-        for o in range(PASSES):
-            words = keep.tile([P, T], I32, name="token_words%d" % o, align_bytes=64)
-            nc.sync.dma_start(words[:], x_words[o].rearrange("p t r -> p (t r)").bitcast(I32))
-            token_words.append(words)
+        token_words = keep.tile([P, PASSES, T], I32, name="token_words", align_bytes=64)
+        nc.sync.dma_start(token_words[:], x_words.rearrange("o p t r -> p o (t r)").bitcast(I32))
 
         out_view = out.rearrange("n (m e u) -> n m e u", m=R, e=E)
 
@@ -67,7 +64,7 @@ def tile_moe_pke_glu_sigmoid_kernel(tc, x_words, x_scales, w1, w3, w2, offs, out
             slot_words = []
             for o in range(PASSES):
                 words = slot_pool.tile([P, GATHER], U32, name="slot_words%d" % o, align_bytes=64)
-                nc.vector.tensor_copy(words[:], token_words[o][:].bitcast(U32).indirect(entries))
+                nc.vector.tensor_copy(words[:], token_words[:, o, :].bitcast(U32).indirect(entries))
                 slot_words.append(words)
             slot_scales = slot_pool.tile([P, GATHER], U8, name="slot_scales", align_bytes=64)
             nc.vector.tensor_copy(slot_scales[:], token_scales[:].bitcast(U8).indirect(entries))

@@ -19,34 +19,35 @@ PACK = 4
 K_PASS = P * PACK
 PASSES = K // K_PASS
 U = C // R
-GATHER = 2 * C
+GATHER = C
 
 
 def tile_moe_pke_glu_sigmoid_kernel(tc, x_words, x_scales, w1, w3, w2, offs, out):
     nc = tc.nc
     with ExitStack() as ctx:
         keep = ctx.enter_context(tc.tile_pool(name="keep", bufs=1))
-        raw_pool = ctx.enter_context(tc.tile_pool(name="raw", bufs=10))
-        stage = ctx.enter_context(tc.tile_pool(name="stage", bufs=10))
+        raw_pool = ctx.enter_context(tc.tile_pool(name="raw", bufs=7))
+        stage = ctx.enter_context(tc.tile_pool(name="stage", bufs=7))
         code_pool = ctx.enter_context(tc.tile_pool(name="codes", bufs=14))
-        slot_pool = ctx.enter_context(tc.tile_pool(name="slots", bufs=2))
+        slot_pool = ctx.enter_context(tc.tile_pool(name="slots", bufs=3))
         work = ctx.enter_context(tc.tile_pool(name="work", bufs=4))
         psum_a = ctx.enter_context(tc.psum_pool(name="psum_a", bufs=3))
         psum_y = ctx.enter_context(tc.psum_pool(name="psum_y", bufs=2))
 
-        def load_pass(w, e, o):
-            raw = raw_pool.tile([P, PACK, H], F32, name="raw", tag="raw")
-            nc.sync.dma_start(raw[:], w[e, o * K_PASS : (o + 1) * K_PASS, :].rearrange("(p j) c -> p j c", j=PACK))
+        def load_passes(w, first, count):
+            raw = raw_pool.tile([P, count, PACK, H], F32, name="raw", tag="raw")
+            rows = w.rearrange("e k c -> (e k) c")[first * K_PASS : (first + count) * K_PASS, :]
+            nc.sync.dma_start(raw[:], rows.rearrange("(o p j) c -> p o j c", p=P, j=PACK))
             return raw
 
-        first_raw = load_pass(w1, 0, 0)
+        first_raw = load_passes(w1, 0, 1)
         offsets = keep.tile([P, E * C // 16], U16, name="offsets")
         nc.sync.dma_start(offsets[:], offs)
 
         token_scales = keep.tile([P, T // 4], I32, name="token_scales", align_bytes=64)
         nc.vector.memset(token_scales[:], 0)
         for q in range(4):
-            nc.gpsimd.dma_start(
+            nc.sync.dma_start(
                 token_scales[32 * q : 32 * q + 4 * PASSES, :],
                 x_scales[:, 4 * q : 4 * q + 4, :].bitcast(I32),
             )
@@ -71,7 +72,7 @@ def tile_moe_pke_glu_sigmoid_kernel(tc, x_words, x_scales, w1, w3, w2, offs, out
             return slot_words, slot_scales
 
         def first_layer_codes(raw, copies):
-            src = raw[:].rearrange("p j (m t) -> p m j t", t=PACK)
+            src = raw.rearrange("p j (m t) -> p m j t", t=PACK)
             tiles = PACK // len(copies)
             parts = []
             for i, copy in enumerate(copies):
@@ -106,12 +107,7 @@ def tile_moe_pke_glu_sigmoid_kernel(tc, x_words, x_scales, w1, w3, w2, offs, out
                     )
             return bank
 
-        def hidden_codes(e, slots):
-            last = e == E - 1
-            w1_codes = [first_layer_codes(first_raw if e == 0 else load_pass(w1, e, 0), on_vector)]
-            w3_codes = [first_layer_codes(load_pass(w3, e, 0), on_scalar)]
-            w1_codes.append(first_layer_codes(load_pass(w1, e, 1), on_both))
-            w3_codes.append(first_layer_codes(load_pass(w3, e, 1), on_both if last else on_scalar))
+        def hidden_codes(e, slots, w1_codes, w3_codes):
             gates = []
             for m in range(R):
                 bank = first_layer_product(w1_codes, slots, (e * C) % GATHER + m * U, "a1")
@@ -134,15 +130,13 @@ def tile_moe_pke_glu_sigmoid_kernel(tc, x_words, x_scales, w1, w3, w2, offs, out
             nc.sync.dma_start(raw[:], w2[e0 : e0 + count].rearrange("e (p j) n -> p e j n", j=PACK))
             codes = code_pool.tile([P, count * N], U32, name="codes", align_bytes=64)
             scales = code_pool.tile([P, count * N], U8, name="scales", align_bytes=64)
-            for d in range(count):
-                copy = nc.vector.tensor_copy if d == 1 else nc.scalar.copy
-                grouped = stage.tile([P, N * PACK], BF16, name="grouped", align_bytes=64)
-                copy(
-                    grouped[:].rearrange("p (c i j) -> p c j i", i=4, j=PACK),
-                    raw[:, d, :, :].rearrange("p j (c i) -> p c j i", i=4),
-                )
-                cols = slice(d * N, (d + 1) * N)
-                nc.vector.quantize_mx(out=codes[:, cols].bitcast(FP8X4), scales=scales[:, cols], in_=grouped[:])
+            copy = nc.vector.tensor_copy if e0 % 4 == 0 else nc.scalar.copy
+            grouped = stage.tile([P, count * N * PACK], BF16, name="grouped", align_bytes=64)
+            copy(
+                grouped[:].rearrange("p (d c i j) -> p d c j i", d=count, i=4, j=PACK),
+                raw[:].rearrange("p d j (c i) -> p d c j i", i=4),
+            )
+            nc.vector.quantize_mx(out=codes[:].bitcast(FP8X4), scales=scales[:], in_=grouped[:])
             return codes, scales
 
         def second_layer_product(weights, d, e0, count, hidden):
@@ -165,11 +159,22 @@ def tile_moe_pke_glu_sigmoid_kernel(tc, x_words, x_scales, w1, w3, w2, offs, out
             nc.sync.dma_start(out_view[:, :, e0 : e0 + count, :], result[:])
 
         hidden = []
-        slots = None
+        slots = gather(0)
+        w1_first = first_layer_codes(first_raw[:, 0], on_scalar)
+        w3_first = first_layer_codes(load_passes(w3, 0, 1)[:, 0], on_scalar)
         for e in range(E):
-            if (e * C) % GATHER == 0:
-                slots = gather(e * C // GATHER)
-            hidden.append(hidden_codes(e, slots))
+            last = e == E - 1
+            if e > 0:
+                slots = gather(e)
+            w1_raw = load_passes(w1, PASSES * e + 1, 1 if last else 2)
+            w1_codes = [w1_first, first_layer_codes(w1_raw[:, 0], on_both if last else on_scalar)]
+            if not last:
+                w1_first = first_layer_codes(w1_raw[:, 1], on_both if e == E - 2 else on_scalar)
+            w3_raw = load_passes(w3, PASSES * e + 1, 1 if last else 2)
+            w3_codes = [w3_first, first_layer_codes(w3_raw[:, 0], on_scalar if last else on_vector)]
+            hidden.append(hidden_codes(e, slots, w1_codes, w3_codes))
+            if not last:
+                w3_first = first_layer_codes(w3_raw[:, 1], on_both)
         for e0 in range(0, E, 2):
             weights = second_layer_codes(e0, 2)
             second_layer_product(weights, 0, e0, 2, hidden)

@@ -19,7 +19,7 @@ PACK = 4
 K_PASS = P * PACK
 PASSES = K // K_PASS
 U = C // R
-GATHER = C
+GATHER = 2 * C
 
 
 def tile_moe_pke_glu_sigmoid_kernel(tc, x_words, x_scales, w1, w3, w2, offs, out):
@@ -27,12 +27,13 @@ def tile_moe_pke_glu_sigmoid_kernel(tc, x_words, x_scales, w1, w3, w2, offs, out
     with ExitStack() as ctx:
         keep = ctx.enter_context(tc.tile_pool(name="keep", bufs=1))
         raw_pool = ctx.enter_context(tc.tile_pool(name="raw", bufs=7))
-        stage = ctx.enter_context(tc.tile_pool(name="stage", bufs=7))
-        code_pool = ctx.enter_context(tc.tile_pool(name="codes", bufs=14))
-        slot_pool = ctx.enter_context(tc.tile_pool(name="slots", bufs=3))
-        work = ctx.enter_context(tc.tile_pool(name="work", bufs=4))
-        psum_a = ctx.enter_context(tc.psum_pool(name="psum_a", bufs=3))
-        psum_y = ctx.enter_context(tc.psum_pool(name="psum_y", bufs=2))
+        stage = ctx.enter_context(tc.tile_pool(name="stage", bufs=6))
+        code_pool = ctx.enter_context(tc.tile_pool(name="codes", bufs=12))
+        slot_pool = ctx.enter_context(tc.tile_pool(name="slots", bufs=E * C // GATHER))
+        work = ctx.enter_context(tc.tile_pool(name="work", bufs=3))
+        psum_a1 = ctx.enter_context(tc.psum_pool(name="psum_a1", bufs=2))
+        psum_a3 = ctx.enter_context(tc.psum_pool(name="psum_a3", bufs=2))
+        psum_y = ctx.enter_context(tc.psum_pool(name="psum_y", bufs=4))
 
         def load_passes(w, first, count):
             raw = raw_pool.tile([P, count, PACK, H], F32, name="raw", tag="raw")
@@ -40,9 +41,14 @@ def tile_moe_pke_glu_sigmoid_kernel(tc, x_words, x_scales, w1, w3, w2, offs, out
             nc.sync.dma_start(raw[:], rows.rearrange("(o p j) c -> p o j c", p=P, j=PACK))
             return raw
 
-        first_raw = load_passes(w1, 0, 1)
         offsets = keep.tile([P, E * C // 16], U16, name="offsets")
         nc.sync.dma_start(offsets[:], offs)
+
+        token_words = []
+        for o in range(PASSES):
+            words = keep.tile([P, T], I32, name="token_words%d" % o, align_bytes=64)
+            nc.sync.dma_start(words[:], x_words[o].rearrange("p t r -> p (t r)").bitcast(I32))
+            token_words.append(words)
 
         token_scales = keep.tile([P, T // 4], I32, name="token_scales", align_bytes=64)
         nc.vector.memset(token_scales[:], 0)
@@ -51,21 +57,20 @@ def tile_moe_pke_glu_sigmoid_kernel(tc, x_words, x_scales, w1, w3, w2, offs, out
                 token_scales[32 * q : 32 * q + 4 * PASSES, :],
                 x_scales[:, 4 * q : 4 * q + 4, :].bitcast(I32),
             )
-        token_words = keep.tile([P, PASSES, T], I32, name="token_words", align_bytes=64)
-        nc.sync.dma_start(token_words[:], x_words.rearrange("o p t r -> p o (t r)").bitcast(I32))
 
         out_view = out.rearrange("n (m e u) -> n m e u", m=R, e=E)
 
         on_vector = [nc.vector.tensor_copy]
         on_scalar = [nc.scalar.copy]
         on_both = on_vector + on_scalar
+        on_vector_halves = on_vector + on_vector
 
         def gather(g):
             entries = offsets[:, g * GATHER // 16 : (g + 1) * GATHER // 16]
             slot_words = []
             for o in range(PASSES):
                 words = slot_pool.tile([P, GATHER], U32, name="slot_words%d" % o, align_bytes=64)
-                nc.vector.tensor_copy(words[:], token_words[:, o, :].bitcast(U32).indirect(entries))
+                nc.vector.tensor_copy(words[:], token_words[o][:].bitcast(U32).indirect(entries))
                 slot_words.append(words)
             slot_scales = slot_pool.tile([P, GATHER], U8, name="slot_scales", align_bytes=64)
             nc.vector.tensor_copy(slot_scales[:], token_scales[:].bitcast(U8).indirect(entries))
@@ -89,48 +94,55 @@ def tile_moe_pke_glu_sigmoid_kernel(tc, x_words, x_scales, w1, w3, w2, offs, out
                     stationary.append((codes[:, cols].bitcast(FP8X4), scales[:, cols]))
             return stationary
 
-        def first_layer_product(weights, slots, first, tag):
-            slot_words, slot_scales = slots
-            bank = psum_a.tile([P, PACK, U], F32, name=tag, tag=tag)
-            cols = slice(first, first + U)
-            for t in range(PACK):
-                for o in range(PASSES):
-                    codes, scales = weights[o][t]
+        def first_layer_pass(banks, weights, e, o):
+            slot_words, slot_scales = all_slots[e * C // GATHER]
+            for m in range(R):
+                first = (e * C) % GATHER + m * U
+                cols = slice(first, first + U)
+                for t in range(PACK):
+                    codes, scales = weights[t]
                     nc.tensor.matmul_mx(
-                        out=bank[:, t, :],
+                        out=banks[m][:, t, :],
                         lhsT=codes,
                         lhsT_scale=scales,
                         rhs=slot_words[o][:, cols].bitcast(FP8X4),
                         rhs_scale=slot_scales[4 * o :, cols],
-                        start=(o == 0),
-                        stop=(o == PASSES - 1),
+                        start=(o == 0 and t == 0),
+                        stop=(o == PASSES - 1 and t == PACK - 1),
                     )
-            return bank
 
-        def hidden_codes(e, slots, w1_codes, w3_codes):
+        def open_sums(pool, tag, weights, e):
+            banks = [pool.tile([P, PACK, U], F32, name=tag, tag=tag) for m in range(R)]
+            first_layer_pass(banks, weights, e, 0)
+            return banks
+
+        def sigmoids(banks, room):
             gates = []
             for m in range(R):
-                bank = first_layer_product(w1_codes, slots, (e * C) % GATHER + m * U, "a1")
-                gate = work.tile([P, U, PACK], F32, name="gate")
-                nc.scalar.activation(gate[:], bank[:].rearrange("p t u -> p u t"), mybir.ActivationFunctionType.Sigmoid)
+                gate = room[:, m, :].rearrange("p (u t) -> p u t", t=PACK)
+                nc.scalar.activation(gate, banks[m][:].rearrange("p t u -> p u t"), mybir.ActivationFunctionType.Sigmoid)
                 gates.append(gate)
+            return gates
+
+        def hidden_codes(e, banks, gates):
             hidden = work.tile([P, C, PACK], BF16, name="hidden", align_bytes=64)
             for m in range(R):
-                bank = first_layer_product(w3_codes, slots, (e * C) % GATHER + m * U, "a3")
                 nc.vector.tensor_tensor(
-                    hidden[:, m * U : (m + 1) * U, :], bank[:].rearrange("p t u -> p u t"), gates[m][:], mybir.AluOpType.mult
+                    hidden[:, m * U : (m + 1) * U, :], banks[m][:].rearrange("p t u -> p u t"), gates[m], mybir.AluOpType.mult
                 )
             codes = keep.tile([P, C], U32, name="hidden_codes%d" % e, align_bytes=64)
             scales = keep.tile([P, C], U8, name="hidden_scales%d" % e, align_bytes=64)
             nc.vector.quantize_mx(out=codes[:].bitcast(FP8X4), scales=scales[:], in_=hidden[:].rearrange("p c t -> p (c t)"))
             return codes, scales
 
-        def second_layer_codes(e0, count):
+        def load_w2(e0, count):
             raw = raw_pool.tile([P, count, PACK, N], F32, name="raw", tag="raw")
             nc.sync.dma_start(raw[:], w2[e0 : e0 + count].rearrange("e (p j) n -> p e j n", j=PACK))
+            return raw
+
+        def second_layer_codes(raw, count, copy):
             codes = code_pool.tile([P, count * N], U32, name="codes", align_bytes=64)
             scales = code_pool.tile([P, count * N], U8, name="scales", align_bytes=64)
-            copy = nc.vector.tensor_copy if e0 % 4 == 0 else nc.scalar.copy
             grouped = stage.tile([P, count * N * PACK], BF16, name="grouped", align_bytes=64)
             copy(
                 grouped[:].rearrange("p (d c i j) -> p d c j i", d=count, i=4, j=PACK),
@@ -139,7 +151,7 @@ def tile_moe_pke_glu_sigmoid_kernel(tc, x_words, x_scales, w1, w3, w2, offs, out
             nc.vector.quantize_mx(out=codes[:].bitcast(FP8X4), scales=scales[:], in_=grouped[:])
             return codes, scales
 
-        def second_layer_product(weights, d, e0, count, hidden):
+        def second_layer_product(weights, d, e0, count, hidden, copy=nc.scalar.copy):
             codes, scales = weights
             bank = psum_y.tile([P, count, R, U], F32, name="y", tag="y")
             for i in range(count):
@@ -155,26 +167,65 @@ def tile_moe_pke_glu_sigmoid_kernel(tc, x_words, x_scales, w1, w3, w2, offs, out
                     stop=True,
                 )
             result = keep.tile([P, R, count, U], F32, name="result%d" % e0)
-            nc.scalar.copy(result[:].rearrange("p m e u -> p e m u"), bank[:])
+            copy(result[:].rearrange("p m e u -> p e m u"), bank[:])
+            return result
+
+        def store(e0, count, result):
             nc.sync.dma_start(out_view[:, :, e0 : e0 + count, :], result[:])
 
         hidden = []
-        slots = gather(0)
-        w1_first = first_layer_codes(first_raw[:, 0], on_scalar)
-        w3_first = first_layer_codes(load_passes(w3, 0, 1)[:, 0], on_scalar)
-        for e in range(E):
+        all_slots = [gather(g) for g in range(E * C // GATHER)]
+        results = []
+
+        def single(w, index, copies):
+            raw = load_passes(w, index, 1)
+            return raw[:, 0], first_layer_codes(raw[:, 0], copies)
+
+        w1_first = single(w1, 0, on_scalar)[1]
+        w3_first = single(w3, 0, on_scalar)[1]
+        for e in range(5):
+            gate_sums = open_sums(psum_a1, "a1", w1_first, e)
+            linear_sums = open_sums(psum_a3, "a3", w3_first, e)
+            w1_raw = load_passes(w1, PASSES * e + 1, 2)
+            first_layer_pass(gate_sums, first_layer_codes(w1_raw[:, 0], on_vector), e, 1)
+            w1_first = first_layer_codes(w1_raw[:, 1], on_scalar)
+            w3_raw = load_passes(w3, PASSES * e + 1, 2)
+            first_layer_pass(linear_sums, first_layer_codes(w3_raw[:, 0], on_vector), e, 1)
+            w3_first = first_layer_codes(w3_raw[:, 1], on_scalar)
+            gates = sigmoids(gate_sums, w3_raw[:, 1])
+            hidden.append(hidden_codes(e, linear_sums, gates))
+            if 2 <= e < 3:
+                e0 = 2 * (e - 2)
+                results.append((e0, 2, second_layer_product(second_layer_codes(load_w2(e0, 2), 2, nc.scalar.copy), 0, e0, 2, hidden)))
+        e = 5
+        gate_sums = open_sums(psum_a1, "a1", w1_first, e)
+        linear_sums = open_sums(psum_a3, "a3", w3_first, e)
+        room, codes = single(w1, PASSES * e + 1, on_vector)
+        first_layer_pass(gate_sums, codes, e, 1)
+        gates = sigmoids(gate_sums, room)
+        first_layer_pass(linear_sums, single(w3, PASSES * e + 1, on_vector)[1], e, 1)
+        hidden.append(hidden_codes(e, linear_sums, gates))
+        pieces = (
+            (2, 2, nc.scalar.copy, nc.scalar.copy),
+            (4, 2, nc.vector.tensor_copy, nc.scalar.copy),
+            (6, 1, nc.scalar.copy, nc.scalar.copy),
+            (7, 1, nc.scalar.copy, nc.vector.tensor_copy),
+        )
+        for e in range(6, E):
             last = e == E - 1
-            if e > 0:
-                slots = gather(e)
-            w1_raw = load_passes(w1, PASSES * e + 1, 1 if last else 2)
-            w1_codes = [w1_first, first_layer_codes(w1_raw[:, 0], on_both if last else on_scalar)]
-            if not last:
-                w1_first = first_layer_codes(w1_raw[:, 1], on_both if e == E - 2 else on_scalar)
-            w3_raw = load_passes(w3, PASSES * e + 1, 1 if last else 2)
-            w3_codes = [w3_first, first_layer_codes(w3_raw[:, 0], on_scalar if last else on_vector)]
-            hidden.append(hidden_codes(e, slots, w1_codes, w3_codes))
-            if not last:
-                w3_first = first_layer_codes(w3_raw[:, 1], on_both)
-        for e0 in range(0, E, 2):
-            weights = second_layer_codes(e0, 2)
-            second_layer_product(weights, 0, e0, 2, hidden)
+            casts = (on_scalar, on_vector, on_scalar, on_vector_halves) if last else (on_scalar, on_vector, on_scalar, on_vector)
+            gate_sums = open_sums(psum_a1, "a1", single(w1, PASSES * e, casts[0])[1], e)
+            room, codes = single(w1, PASSES * e + 1, casts[1])
+            first_layer_pass(gate_sums, codes, e, 1)
+            later_room, codes = single(w3, PASSES * e, casts[2])
+            gates = sigmoids(gate_sums, room)
+            linear_sums = open_sums(psum_a3, "a3", codes, e)
+            first_layer_pass(linear_sums, single(w3, PASSES * e + 1, casts[3])[1], e, 1)
+            if last:
+                for e0, count, cast, copy in pieces[:2]:
+                    results.append((e0, count, second_layer_product(second_layer_codes(load_w2(e0, count), count, cast), 0, e0, count, hidden, copy)))
+            hidden.append(hidden_codes(e, linear_sums, gates))
+        for e0, count, cast, copy in pieces[2:]:
+            results.append((e0, count, second_layer_product(second_layer_codes(load_w2(e0, count), count, cast), 0, e0, count, hidden, copy)))
+        for e0, count, result in results:
+            store(e0, count, result)

@@ -27,7 +27,7 @@ def tile_moe_pke_glu_sigmoid_kernel(tc, x_words, x_scales, w1, w3, w2, offs, out
     with ExitStack() as ctx:
         keep = ctx.enter_context(tc.tile_pool(name="keep", bufs=1))
         raw_pool = ctx.enter_context(tc.tile_pool(name="raw", bufs=7))
-        stage = ctx.enter_context(tc.tile_pool(name="stage", bufs=6))
+        stage = ctx.enter_context(tc.tile_pool(name="stage", bufs=8))
         code_pool = ctx.enter_context(tc.tile_pool(name="codes", bufs=12))
         slot_pool = ctx.enter_context(tc.tile_pool(name="slots", bufs=E * C // GATHER))
         work = ctx.enter_context(tc.tile_pool(name="work", bufs=3))
@@ -149,14 +149,14 @@ def tile_moe_pke_glu_sigmoid_kernel(tc, x_words, x_scales, w1, w3, w2, offs, out
                 raw[:].rearrange("p d j (c i) -> p d c j i", i=4),
             )
             nc.vector.quantize_mx(out=codes[:].bitcast(FP8X4), scales=scales[:], in_=grouped[:])
-            return codes, scales
+            return codes, scales, grouped
 
         def second_layer_product(weights, d, e0, count, hidden, copy=nc.scalar.copy):
-            codes, scales = weights
             bank = psum_y.tile([P, count, R, U], F32, name="y", tag="y")
             for i in range(count):
+                codes, scales = weights[i][:2] if d else weights[:2]
                 h_codes, h_scales = hidden[e0 + i]
-                cols = slice((d + i) * N, (d + i + 1) * N)
+                cols = slice(0, N) if d else slice(i * N, (i + 1) * N)
                 nc.tensor.matmul_mx(
                     out=bank[:, i, :, :].rearrange("p m u -> p (m u)"),
                     lhsT=codes[:, cols].bitcast(FP8X4),
@@ -177,55 +177,51 @@ def tile_moe_pke_glu_sigmoid_kernel(tc, x_words, x_scales, w1, w3, w2, offs, out
         all_slots = [gather(g) for g in range(E * C // GATHER)]
         results = []
 
+        def second_layer(e0, count, cast, copy):
+            results.append((e0, count, second_layer_product(second_layer_codes(load_w2(e0, count), count, cast), 0, e0, count, hidden, copy)))
+
         def single(w, index, copies):
             raw = load_passes(w, index, 1)
             return raw[:, 0], first_layer_codes(raw[:, 0], copies)
 
-        w1_first = single(w1, 0, on_scalar)[1]
-        w3_first = single(w3, 0, on_scalar)[1]
-        for e in range(5):
-            gate_sums = open_sums(psum_a1, "a1", w1_first, e)
-            linear_sums = open_sums(psum_a3, "a3", w3_first, e)
-            w1_raw = load_passes(w1, PASSES * e + 1, 2)
-            first_layer_pass(gate_sums, first_layer_codes(w1_raw[:, 0], on_vector), e, 1)
-            w1_first = first_layer_codes(w1_raw[:, 1], on_scalar)
-            w3_raw = load_passes(w3, PASSES * e + 1, 2)
-            first_layer_pass(linear_sums, first_layer_codes(w3_raw[:, 0], on_vector), e, 1)
-            w3_first = first_layer_codes(w3_raw[:, 1], on_scalar)
-            gates = sigmoids(gate_sums, w3_raw[:, 1])
-            hidden.append(hidden_codes(e, linear_sums, gates))
-            if 2 <= e < 3:
-                e0 = 2 * (e - 2)
-                results.append((e0, 2, second_layer_product(second_layer_codes(load_w2(e0, 2), 2, nc.scalar.copy), 0, e0, 2, hidden)))
-        e = 5
-        gate_sums = open_sums(psum_a1, "a1", w1_first, e)
-        linear_sums = open_sums(psum_a3, "a3", w3_first, e)
-        room, codes = single(w1, PASSES * e + 1, on_vector)
+        for e in range(7):
+            w1_raw = load_passes(w1, PASSES * e, 2)
+            gate_sums = open_sums(psum_a1, "a1", first_layer_codes(w1_raw[:, 0], on_both), e)
+            first_layer_pass(gate_sums, first_layer_codes(w1_raw[:, 1], on_scalar), e, 1)
+            w3_raw = load_passes(w3, PASSES * e, 2)
+            linear_sums = open_sums(psum_a3, "a3", first_layer_codes(w3_raw[:, 0], on_vector_halves), e)
+            first_layer_pass(linear_sums, first_layer_codes(w3_raw[:, 1], on_scalar), e, 1)
+            hidden.append(hidden_codes(e, linear_sums, sigmoids(gate_sums, w3_raw[:, 1])))
+            if 2 <= e < 4:
+                second_layer(2 * (e - 2), 2, nc.scalar.copy, nc.scalar.copy)
+        e = 7
+        gate_sums = open_sums(psum_a1, "a1", single(w1, PASSES * e, on_both)[1], e)
+        room, codes = single(w1, PASSES * e + 1, on_scalar)
         first_layer_pass(gate_sums, codes, e, 1)
+        later_room, codes = single(w3, PASSES * e, on_both)
         gates = sigmoids(gate_sums, room)
-        first_layer_pass(linear_sums, single(w3, PASSES * e + 1, on_vector)[1], e, 1)
-        hidden.append(hidden_codes(e, linear_sums, gates))
-        pieces = (
-            (2, 2, nc.scalar.copy, nc.scalar.copy),
-            (4, 2, nc.vector.tensor_copy, nc.scalar.copy),
-            (6, 1, nc.scalar.copy, nc.scalar.copy),
-            (7, 1, nc.scalar.copy, nc.vector.tensor_copy),
-        )
-        for e in range(6, E):
-            last = e == E - 1
-            casts = (on_scalar, on_vector, on_scalar, on_vector_halves) if last else (on_scalar, on_vector, on_scalar, on_vector)
-            gate_sums = open_sums(psum_a1, "a1", single(w1, PASSES * e, casts[0])[1], e)
-            room, codes = single(w1, PASSES * e + 1, casts[1])
-            first_layer_pass(gate_sums, codes, e, 1)
-            later_room, codes = single(w3, PASSES * e, casts[2])
-            gates = sigmoids(gate_sums, room)
-            linear_sums = open_sums(psum_a3, "a3", codes, e)
-            first_layer_pass(linear_sums, single(w3, PASSES * e + 1, casts[3])[1], e, 1)
-            if last:
-                for e0, count, cast, copy in pieces[:2]:
-                    results.append((e0, count, second_layer_product(second_layer_codes(load_w2(e0, count), count, cast), 0, e0, count, hidden, copy)))
-            hidden.append(hidden_codes(e, linear_sums, gates))
-        for e0, count, cast, copy in pieces[2:]:
-            results.append((e0, count, second_layer_product(second_layer_codes(load_w2(e0, count), count, cast), 0, e0, count, hidden, copy)))
+        linear_sums = open_sums(psum_a3, "a3", codes, e)
+        first_layer_pass(linear_sums, single(w3, PASSES * e + 1, on_vector_halves)[1], e, 1)
+        late = [second_layer_codes(load_w2(x, 1), 1, (nc.scalar.copy, nc.scalar.copy, nc.scalar.copy, nc.scalar.copy,)[x - 4]) for x in range(4, E)]
+        results.append((4, 2, second_layer_product(late[0 : 2], 1, 4, 2, hidden, nc.scalar.copy)))
+        results.append((6, 1, second_layer_product(late[2 : 3], 1, 6, 1, hidden, nc.scalar.copy)))
+        w2_codes, w2_scales = late[-1][:2]
+        last_results = []
+        parts = []
+        for m in range(R):
+            part = work.tile([P, U * PACK], BF16, name="hidden", align_bytes=64) if m == 0 else work.tile([P, U * PACK], BF16, name="hidden", align_bytes=64)
+            nc.vector.tensor_tensor(part[:].rearrange("p (u t) -> p u t", t=PACK), linear_sums[m][:].rearrange("p t u -> p u t"), gates[m], mybir.AluOpType.mult)
+            parts.append(part)
+        for m in range(R):
+            codes = keep.tile([P, U], U32, name="last_codes%d" % m, align_bytes=64)
+            scales = keep.tile([P, U], U8, name="last_scales%d" % m, align_bytes=64)
+            nc.vector.quantize_mx(out=codes[:].bitcast(FP8X4), scales=scales[:], in_=parts[m][:])
+            bank = psum_y.tile([P, U], F32, name="y", tag="y")
+            nc.tensor.matmul_mx(out=bank[:], lhsT=w2_codes[:].bitcast(FP8X4), lhsT_scale=w2_scales[:], rhs=codes[:].bitcast(FP8X4), rhs_scale=scales[:], start=True, stop=True)
+            result = keep.tile([P, U], F32, name="last_result%d" % m)
+            (nc.scalar.copy, nc.vector.tensor_copy)[m](result[:], bank[:])
+            last_results.append(result)
         for e0, count, result in results:
             store(e0, count, result)
+        for m in range(R):
+            nc.sync.dma_start(out_view[:, m, E - 1, :], last_results[m][:])

@@ -20,6 +20,9 @@ K_PASS = P * PACK
 PASSES = K // K_PASS
 U = C // R
 GATHER = 2 * C
+LAST = E - 1
+LATE_W2 = 4
+FIRST_PAIR_AT = 2
 
 
 def tile_moe_pke_glu_sigmoid_kernel(tc, x_words, x_scales, w1, w3, w2, offs, out):
@@ -31,15 +34,9 @@ def tile_moe_pke_glu_sigmoid_kernel(tc, x_words, x_scales, w1, w3, w2, offs, out
         code_pool = ctx.enter_context(tc.tile_pool(name="codes", bufs=12))
         slot_pool = ctx.enter_context(tc.tile_pool(name="slots", bufs=E * C // GATHER))
         work = ctx.enter_context(tc.tile_pool(name="work", bufs=3))
-        psum_a1 = ctx.enter_context(tc.psum_pool(name="psum_a1", bufs=2))
-        psum_a3 = ctx.enter_context(tc.psum_pool(name="psum_a3", bufs=2))
+        psum_gate = ctx.enter_context(tc.psum_pool(name="psum_gate", bufs=R))
+        psum_linear = ctx.enter_context(tc.psum_pool(name="psum_linear", bufs=R))
         psum_y = ctx.enter_context(tc.psum_pool(name="psum_y", bufs=4))
-
-        def load_passes(w, first, count):
-            raw = raw_pool.tile([P, count, PACK, H], F32, name="raw", tag="raw")
-            rows = w.rearrange("e k c -> (e k) c")[first * K_PASS : (first + count) * K_PASS, :]
-            nc.sync.dma_start(raw[:], rows.rearrange("(o p j) c -> p o j c", p=P, j=PACK))
-            return raw
 
         offsets = keep.tile([P, E * C // 16], U16, name="offsets")
         nc.sync.dma_start(offsets[:], offs)
@@ -62,8 +59,8 @@ def tile_moe_pke_glu_sigmoid_kernel(tc, x_words, x_scales, w1, w3, w2, offs, out
 
         on_vector = [nc.vector.tensor_copy]
         on_scalar = [nc.scalar.copy]
-        on_both = on_vector + on_scalar
-        on_vector_halves = on_vector + on_vector
+        on_both = [nc.vector.tensor_copy, nc.scalar.copy]
+        on_vector_by_pairs = [nc.vector.tensor_copy, nc.vector.tensor_copy]
 
         def gather(g):
             entries = offsets[:, g * GATHER // 16 : (g + 1) * GATHER // 16]
@@ -76,31 +73,42 @@ def tile_moe_pke_glu_sigmoid_kernel(tc, x_words, x_scales, w1, w3, w2, offs, out
             nc.vector.tensor_copy(slot_scales[:], token_scales[:].bitcast(U8).indirect(entries))
             return slot_words, slot_scales
 
+        def load_passes(w, e, first, count):
+            raw = raw_pool.tile([P, count, PACK, H], F32, name="raw", tag="raw")
+            rows = w[e, first * K_PASS : (first + count) * K_PASS, :]
+            nc.sync.dma_start(raw[:], rows.rearrange("(o p j) c -> p o j c", p=P, j=PACK))
+            return raw
+
+        def quantise(pool, values, tag=""):
+            columns = values.shape[1] // PACK
+            codes = pool.tile([P, columns], U32, name="codes" + tag, align_bytes=64)
+            scales = pool.tile([P, columns], U8, name="scales" + tag, align_bytes=64)
+            nc.vector.quantize_mx(out=codes[:].bitcast(FP8X4), scales=scales[:], in_=values)
+            return codes, scales
+
         def first_layer_codes(raw, copies):
             src = raw.rearrange("p j (m t) -> p m j t", t=PACK)
-            tiles = PACK // len(copies)
-            parts = []
-            for i, copy in enumerate(copies):
-                grouped = stage.tile([P, tiles * P * PACK], BF16, name="grouped", align_bytes=64)
-                copy(grouped[:].rearrange("p (t m j) -> p m j t", t=tiles, j=PACK), src[:, :, :, i * tiles : (i + 1) * tiles])
-                parts.append(grouped)
+            groups = PACK // len(copies)
+            rounded = []
+            for n, copy in enumerate(copies):
+                grouped = stage.tile([P, groups * P * PACK], BF16, name="grouped", align_bytes=64)
+                copy(grouped[:].rearrange("p (t m j) -> p m j t", t=groups, j=PACK), src[:, :, :, n * groups : (n + 1) * groups])
+                rounded.append(grouped)
             stationary = []
-            for grouped in parts:
-                codes = code_pool.tile([P, tiles * P], U32, name="codes", align_bytes=64)
-                scales = code_pool.tile([P, tiles * P], U8, name="scales", align_bytes=64)
-                nc.vector.quantize_mx(out=codes[:].bitcast(FP8X4), scales=scales[:], in_=grouped[:])
-                for t in range(tiles):
+            for grouped in rounded:
+                codes, scales = quantise(code_pool, grouped[:])
+                for t in range(groups):
                     cols = slice(t * P, (t + 1) * P)
                     stationary.append((codes[:, cols].bitcast(FP8X4), scales[:, cols]))
             return stationary
 
-        def first_layer_pass(banks, weights, e, o):
+        def first_layer_pass(banks, stationary, e, o):
             slot_words, slot_scales = all_slots[e * C // GATHER]
             for m in range(R):
                 first = (e * C) % GATHER + m * U
                 cols = slice(first, first + U)
                 for t in range(PACK):
-                    codes, scales = weights[t]
+                    codes, scales = stationary[t]
                     nc.tensor.matmul_mx(
                         out=banks[m][:, t, :],
                         lhsT=codes,
@@ -111,117 +119,99 @@ def tile_moe_pke_glu_sigmoid_kernel(tc, x_words, x_scales, w1, w3, w2, offs, out
                         stop=(o == PASSES - 1 and t == PACK - 1),
                     )
 
-        def open_sums(pool, tag, weights, e):
-            banks = [pool.tile([P, PACK, U], F32, name=tag, tag=tag) for m in range(R)]
-            first_layer_pass(banks, weights, e, 0)
+        def open_sums(pool, stationary, e):
+            banks = [pool.tile([P, PACK, U], F32, name="sums") for m in range(R)]
+            first_layer_pass(banks, stationary, e, 0)
             return banks
 
-        def sigmoids(banks, room):
+        def sigmoids(banks, spent):
             gates = []
             for m in range(R):
-                gate = room[:, m, :].rearrange("p (u t) -> p u t", t=PACK)
+                gate = spent[:, m, :].rearrange("p (u t) -> p u t", t=PACK)
                 nc.scalar.activation(gate, banks[m][:].rearrange("p t u -> p u t"), mybir.ActivationFunctionType.Sigmoid)
                 gates.append(gate)
             return gates
 
-        def hidden_codes(e, banks, gates):
-            hidden = work.tile([P, C, PACK], BF16, name="hidden", align_bytes=64)
-            for m in range(R):
-                nc.vector.tensor_tensor(
-                    hidden[:, m * U : (m + 1) * U, :], banks[m][:].rearrange("p t u -> p u t"), gates[m], mybir.AluOpType.mult
-                )
-            codes = keep.tile([P, C], U32, name="hidden_codes%d" % e, align_bytes=64)
-            scales = keep.tile([P, C], U8, name="hidden_scales%d" % e, align_bytes=64)
-            nc.vector.quantize_mx(out=codes[:].bitcast(FP8X4), scales=scales[:], in_=hidden[:].rearrange("p c t -> p (c t)"))
-            return codes, scales
+        def gated_product(h, bank, gate):
+            nc.vector.tensor_tensor(h, bank[:].rearrange("p t u -> p u t"), gate, mybir.AluOpType.mult)
 
-        def load_w2(e0, count):
+        def hidden_codes(e, banks, gates):
+            h = work.tile([P, C, PACK], BF16, name="h", align_bytes=64)
+            for m in range(R):
+                gated_product(h[:, m * U : (m + 1) * U, :], banks[m], gates[m])
+            return quantise(keep, h[:].rearrange("p c t -> p (c t)"), "_h%d" % e)
+
+        def second_layer_codes(e0, count):
             raw = raw_pool.tile([P, count, PACK, N], F32, name="raw", tag="raw")
             nc.sync.dma_start(raw[:], w2[e0 : e0 + count].rearrange("e (p j) n -> p e j n", j=PACK))
-            return raw
-
-        def second_layer_codes(raw, count, copy):
-            codes = code_pool.tile([P, count * N], U32, name="codes", align_bytes=64)
-            scales = code_pool.tile([P, count * N], U8, name="scales", align_bytes=64)
             grouped = stage.tile([P, count * N * PACK], BF16, name="grouped", align_bytes=64)
-            copy(
-                grouped[:].rearrange("p (d c i j) -> p d c j i", d=count, i=4, j=PACK),
-                raw[:].rearrange("p d j (c i) -> p d c j i", i=4),
+            nc.scalar.copy(
+                grouped[:].rearrange("p (d c b j) -> p d c j b", d=count, b=4, j=PACK),
+                raw[:].rearrange("p d j (c b) -> p d c j b", b=4),
             )
-            nc.vector.quantize_mx(out=codes[:].bitcast(FP8X4), scales=scales[:], in_=grouped[:])
-            return codes, scales, grouped
+            codes, scales = quantise(code_pool, grouped[:])
+            return [(codes[:, d * N : (d + 1) * N], scales[:, d * N : (d + 1) * N]) for d in range(count)]
 
-        def second_layer_product(weights, d, e0, count, hidden, copy=nc.scalar.copy):
+        def second_layer_matmul(y, stationary, moving):
+            nc.tensor.matmul_mx(
+                out=y,
+                lhsT=stationary[0].bitcast(FP8X4),
+                lhsT_scale=stationary[1],
+                rhs=moving[0][:].bitcast(FP8X4),
+                rhs_scale=moving[1][:],
+                start=True,
+                stop=True,
+            )
+
+        def second_layer_results(e0, w2_codes):
+            count = len(w2_codes)
             bank = psum_y.tile([P, count, R, U], F32, name="y", tag="y")
-            for i in range(count):
-                codes, scales = weights[i][:2] if d else weights[:2]
-                h_codes, h_scales = hidden[e0 + i]
-                cols = slice(0, N) if d else slice(i * N, (i + 1) * N)
-                nc.tensor.matmul_mx(
-                    out=bank[:, i, :, :].rearrange("p m u -> p (m u)"),
-                    lhsT=codes[:, cols].bitcast(FP8X4),
-                    lhsT_scale=scales[:, cols],
-                    rhs=h_codes[:].bitcast(FP8X4),
-                    rhs_scale=h_scales[:],
-                    start=True,
-                    stop=True,
-                )
+            for d in range(count):
+                second_layer_matmul(bank[:, d, :, :].rearrange("p m u -> p (m u)"), w2_codes[d], hidden[e0 + d])
             result = keep.tile([P, R, count, U], F32, name="result%d" % e0)
-            copy(result[:].rearrange("p m e u -> p e m u"), bank[:])
-            return result
-
-        def store(e0, count, result):
-            nc.sync.dma_start(out_view[:, :, e0 : e0 + count, :], result[:])
+            nc.scalar.copy(result[:].rearrange("p m e u -> p e m u"), bank[:])
+            stores.append((out_view[:, :, e0 : e0 + count, :], result))
 
         hidden = []
+        stores = []
         all_slots = [gather(g) for g in range(E * C // GATHER)]
-        results = []
 
-        def second_layer(e0, count, cast, copy):
-            results.append((e0, count, second_layer_product(second_layer_codes(load_w2(e0, count), count, cast), 0, e0, count, hidden, copy)))
-
-        def single(w, index, copies):
-            raw = load_passes(w, index, 1)
-            return raw[:, 0], first_layer_codes(raw[:, 0], copies)
-
-        for e in range(7):
-            w1_raw = load_passes(w1, PASSES * e, 2)
-            gate_sums = open_sums(psum_a1, "a1", first_layer_codes(w1_raw[:, 0], on_both), e)
+        for e in range(LAST):
+            w1_raw = load_passes(w1, e, 0, PASSES)
+            gate_sums = open_sums(psum_gate, first_layer_codes(w1_raw[:, 0], on_both), e)
             first_layer_pass(gate_sums, first_layer_codes(w1_raw[:, 1], on_scalar), e, 1)
-            w3_raw = load_passes(w3, PASSES * e, 2)
-            linear_sums = open_sums(psum_a3, "a3", first_layer_codes(w3_raw[:, 0], on_vector_halves), e)
+            w3_raw = load_passes(w3, e, 0, PASSES)
+            linear_sums = open_sums(psum_linear, first_layer_codes(w3_raw[:, 0], on_vector_by_pairs), e)
             first_layer_pass(linear_sums, first_layer_codes(w3_raw[:, 1], on_scalar), e, 1)
             hidden.append(hidden_codes(e, linear_sums, sigmoids(gate_sums, w3_raw[:, 1])))
-            if 2 <= e < 4:
-                second_layer(2 * (e - 2), 2, nc.scalar.copy, nc.scalar.copy)
-        e = 7
-        gate_sums = open_sums(psum_a1, "a1", single(w1, PASSES * e, on_both)[1], e)
-        room, codes = single(w1, PASSES * e + 1, on_scalar)
-        first_layer_pass(gate_sums, codes, e, 1)
-        later_room, codes = single(w3, PASSES * e, on_both)
-        gates = sigmoids(gate_sums, room)
-        linear_sums = open_sums(psum_a3, "a3", codes, e)
-        first_layer_pass(linear_sums, single(w3, PASSES * e + 1, on_vector_halves)[1], e, 1)
-        late = [second_layer_codes(load_w2(x, 1), 1, (nc.scalar.copy, nc.scalar.copy, nc.scalar.copy, nc.scalar.copy,)[x - 4]) for x in range(4, E)]
-        results.append((4, 2, second_layer_product(late[0 : 2], 1, 4, 2, hidden, nc.scalar.copy)))
-        results.append((6, 1, second_layer_product(late[2 : 3], 1, 6, 1, hidden, nc.scalar.copy)))
-        w2_codes, w2_scales = late[-1][:2]
-        last_results = []
-        parts = []
+            if FIRST_PAIR_AT <= e < FIRST_PAIR_AT + LATE_W2 // 2:
+                e0 = 2 * (e - FIRST_PAIR_AT)
+                second_layer_results(e0, second_layer_codes(e0, 2))
+
+        gate_sums = open_sums(psum_gate, first_layer_codes(load_passes(w1, LAST, 0, 1)[:, 0], on_vector), LAST)
+        w1_raw = load_passes(w1, LAST, 1, 1)
+        first_layer_pass(gate_sums, first_layer_codes(w1_raw[:, 0], on_scalar), LAST, 1)
+        stationary = first_layer_codes(load_passes(w3, LAST, 0, 1)[:, 0], on_both)
+        gates = sigmoids(gate_sums, w1_raw[:, 0])
+        linear_sums = open_sums(psum_linear, stationary, LAST)
+        first_layer_pass(linear_sums, first_layer_codes(load_passes(w3, LAST, 1, 1)[:, 0], on_vector_by_pairs), LAST, 1)
+
+        late_codes = {e: second_layer_codes(e, 1)[0] for e in range(LATE_W2, E)}
+        for e0 in range(LATE_W2, LAST, 2):
+            second_layer_results(e0, [late_codes[e] for e in range(e0, min(e0 + 2, LAST))])
+
+        h_ranks = []
         for m in range(R):
-            part = work.tile([P, U * PACK], BF16, name="hidden", align_bytes=64) if m == 0 else work.tile([P, U * PACK], BF16, name="hidden", align_bytes=64)
-            nc.vector.tensor_tensor(part[:].rearrange("p (u t) -> p u t", t=PACK), linear_sums[m][:].rearrange("p t u -> p u t"), gates[m], mybir.AluOpType.mult)
-            parts.append(part)
-        for m in range(R):
-            codes = keep.tile([P, U], U32, name="last_codes%d" % m, align_bytes=64)
-            scales = keep.tile([P, U], U8, name="last_scales%d" % m, align_bytes=64)
-            nc.vector.quantize_mx(out=codes[:].bitcast(FP8X4), scales=scales[:], in_=parts[m][:])
+            h = work.tile([P, U * PACK], BF16, name="h", align_bytes=64)
+            gated_product(h[:].rearrange("p (u t) -> p u t", t=PACK), linear_sums[m], gates[m])
+            h_ranks.append(h)
+        for m, copy in enumerate((nc.scalar.copy, nc.vector.tensor_copy)):
+            rank_codes = quantise(keep, h_ranks[m][:], "_rank%d" % m)
             bank = psum_y.tile([P, U], F32, name="y", tag="y")
-            nc.tensor.matmul_mx(out=bank[:], lhsT=w2_codes[:].bitcast(FP8X4), lhsT_scale=w2_scales[:], rhs=codes[:].bitcast(FP8X4), rhs_scale=scales[:], start=True, stop=True)
-            result = keep.tile([P, U], F32, name="last_result%d" % m)
-            (nc.scalar.copy, nc.vector.tensor_copy)[m](result[:], bank[:])
-            last_results.append(result)
-        for e0, count, result in results:
-            store(e0, count, result)
-        for m in range(R):
-            nc.sync.dma_start(out_view[:, m, E - 1, :], last_results[m][:])
+            second_layer_matmul(bank[:], late_codes[LAST], rank_codes)
+            result = keep.tile([P, U], F32, name="rank_result%d" % m)
+            copy(result[:], bank[:])
+            stores.append((out_view[:, m, LAST, :], result))
+
+        for place, result in stores:
+            nc.sync.dma_start(place, result[:])

@@ -43,11 +43,11 @@ def tile_moe_pke_glu_sigmoid_kernel(tc, x_words, x_scales, w1, w3, w2, offs, out
 
         token_words = []
         for o in range(PASSES):
-            words = keep.tile([P, T], I32, name="token_words%d" % o, align_bytes=64)
+            words = keep.tile([P, T], I32, name="token_words%d" % o, align_bytes=256)
             nc.sync.dma_start(words[:], x_words[o].rearrange("p t r -> p (t r)").bitcast(I32))
             token_words.append(words)
 
-        token_scales = keep.tile([P, T // 4], I32, name="token_scales", align_bytes=64)
+        token_scales = keep.tile([P, T // 4], I32, name="token_scales", align_bytes=256)
         nc.vector.memset(token_scales[:], 0)
         for q in range(4):
             nc.sync.dma_start(
@@ -74,7 +74,7 @@ def tile_moe_pke_glu_sigmoid_kernel(tc, x_words, x_scales, w1, w3, w2, offs, out
             return slot_words, slot_scales
 
         def load_passes(w, e, first, count):
-            raw = raw_pool.tile([P, count, PACK, H], F32, name="raw", tag="raw")
+            raw = raw_pool.tile([P, count, PACK, H], F32, name="raw", tag="raw", align_bytes=256)
             rows = w[e, first * K_PASS : (first + count) * K_PASS, :]
             nc.sync.dma_start(raw[:], rows.rearrange("(o p j) c -> p o j c", p=P, j=PACK))
             return raw
@@ -142,7 +142,7 @@ def tile_moe_pke_glu_sigmoid_kernel(tc, x_words, x_scales, w1, w3, w2, offs, out
             return quantise(keep, h[:].rearrange("p c t -> p (c t)"), "_h%d" % e)
 
         def second_layer_codes(e0, count):
-            raw = raw_pool.tile([P, count, PACK, N], F32, name="raw", tag="raw")
+            raw = raw_pool.tile([P, count, PACK, N], F32, name="raw", tag="raw", align_bytes=256)
             nc.sync.dma_start(raw[:], w2[e0 : e0 + count].rearrange("e (p j) n -> p e j n", j=PACK))
             grouped = stage.tile([P, count * N * PACK], BF16, name="grouped", align_bytes=64)
             nc.scalar.copy(
@@ -168,7 +168,7 @@ def tile_moe_pke_glu_sigmoid_kernel(tc, x_words, x_scales, w1, w3, w2, offs, out
             bank = psum_y.tile([P, count, R, U], F32, name="y", tag="y")
             for d in range(count):
                 second_layer_matmul(bank[:, d, :, :].rearrange("p m u -> p (m u)"), w2_codes[d], hidden[e0 + d])
-            result = keep.tile([P, R, count, U], F32, name="result%d" % e0)
+            result = keep.tile([P, R, count, U], F32, name="result%d" % e0, align_bytes=256)
             nc.scalar.copy(result[:].rearrange("p m e u -> p e m u"), bank[:])
             stores.append((out_view[:, :, e0 : e0 + count, :], result))
 
@@ -209,7 +209,7 @@ def tile_moe_pke_glu_sigmoid_kernel(tc, x_words, x_scales, w1, w3, w2, offs, out
             rank_codes = quantise(keep, h_ranks[m][:], "_rank%d" % m)
             bank = psum_y.tile([P, U], F32, name="y", tag="y")
             second_layer_matmul(bank[:], late_codes[LAST], rank_codes)
-            result = keep.tile([P, U], F32, name="rank_result%d" % m)
+            result = keep.tile([P, U], F32, name="rank_result%d" % m, align_bytes=256)
             copy(result[:], bank[:])
             stores.append((out_view[:, m, LAST, :], result))
 

@@ -38,7 +38,7 @@ def tile_moe_pke_glu_sigmoid_kernel(tc, x_words, x_scales, w1, w3, w2, offs, out
         psum_linear = ctx.enter_context(tc.psum_pool(name="psum_linear", bufs=R))
         psum_y = ctx.enter_context(tc.psum_pool(name="psum_y", bufs=4))
 
-        offsets = keep.tile([P, E * C // 16], U16, name="offsets")
+        offsets = keep.tile([P, E * C // 16], U16, name="offsets", align_bytes=256)
         nc.sync.dma_start(offsets[:], offs)
 
         token_words = []
@@ -86,7 +86,7 @@ def tile_moe_pke_glu_sigmoid_kernel(tc, x_words, x_scales, w1, w3, w2, offs, out
             nc.vector.quantize_mx(out=codes[:].bitcast(FP8X4), scales=scales[:], in_=values)
             return codes, scales
 
-        def first_layer_codes(raw, copies):
+        def round_pass(raw, copies):
             src = raw.rearrange("p j (m t) -> p m j t", t=PACK)
             groups = PACK // len(copies)
             rounded = []
@@ -94,6 +94,10 @@ def tile_moe_pke_glu_sigmoid_kernel(tc, x_words, x_scales, w1, w3, w2, offs, out
                 grouped = stage.tile([P, groups * P * PACK], BF16, name="grouped", align_bytes=64)
                 copy(grouped[:].rearrange("p (t m j) -> p m j t", t=groups, j=PACK), src[:, :, :, n * groups : (n + 1) * groups])
                 rounded.append(grouped)
+            return rounded
+
+        def pass_codes(rounded):
+            groups = PACK // len(rounded)
             stationary = []
             for grouped in rounded:
                 codes, scales = quantise(code_pool, grouped[:])
@@ -101,6 +105,9 @@ def tile_moe_pke_glu_sigmoid_kernel(tc, x_words, x_scales, w1, w3, w2, offs, out
                     cols = slice(t * P, (t + 1) * P)
                     stationary.append((codes[:, cols].bitcast(FP8X4), scales[:, cols]))
             return stationary
+
+        def first_layer_codes(raw, copies):
+            return pass_codes(round_pass(raw, copies))
 
         def first_layer_pass(banks, stationary, e, o):
             slot_words, slot_scales = all_slots[e * C // GATHER]
@@ -176,19 +183,38 @@ def tile_moe_pke_glu_sigmoid_kernel(tc, x_words, x_scales, w1, w3, w2, offs, out
         stores = []
         all_slots = [gather(g) for g in range(E * C // GATHER)]
 
+        def products(spent, banks, gates):
+            h = spent[:, 0, :].bitcast(BF16)
+            for m in range(R):
+                gated_product(h[:, m * U * PACK : (m + 1) * U * PACK].rearrange("p (u t) -> p u t", t=PACK), banks[m], gates[m])
+            return h
+
+        waiting = None
         for e in range(LAST):
             w1_raw = load_passes(w1, e, 0, PASSES)
-            gate_sums = open_sums(psum_gate, first_layer_codes(w1_raw[:, 0], on_both), e)
-            first_layer_pass(gate_sums, first_layer_codes(w1_raw[:, 1], on_scalar), e, 1)
+            first = on_scalar if e == 0 else on_vector
+            rounded = [round_pass(w1_raw[:, 0], first), round_pass(w1_raw[:, 1], on_scalar)]
+            if e == 1:
+                waiting = (linear_sums, sigmoids(gate_sums, w1_raw[:, 1]))
+            if waiting:
+                h = products(w1_raw[:, 0], *waiting)
+            gate_sums = open_sums(psum_gate, pass_codes(rounded[0]), e)
+            first_layer_pass(gate_sums, pass_codes(rounded[1]), e, 1)
+            if waiting:
+                hidden.append(quantise(keep, h, "_h%d" % (e - 1)))
             w3_raw = load_passes(w3, e, 0, PASSES)
-            linear_sums = open_sums(psum_linear, first_layer_codes(w3_raw[:, 0], on_vector_by_pairs), e)
+            linear_sums = open_sums(psum_linear, first_layer_codes(w3_raw[:, 0], first), e)
             first_layer_pass(linear_sums, first_layer_codes(w3_raw[:, 1], on_scalar), e, 1)
-            hidden.append(hidden_codes(e, linear_sums, sigmoids(gate_sums, w3_raw[:, 1])))
-            if FIRST_PAIR_AT <= e < FIRST_PAIR_AT + LATE_W2 // 2:
-                e0 = 2 * (e - FIRST_PAIR_AT)
-                second_layer_results(e0, second_layer_codes(e0, 2))
+            if e > 0:
+                waiting = (linear_sums, sigmoids(gate_sums, w3_raw[:, 1]))
+            if e in (2, 4):
+                second_layer_results(e - 2, second_layer_codes(e - 2, 2))
 
-        gate_sums = open_sums(psum_gate, first_layer_codes(load_passes(w1, LAST, 0, 1)[:, 0], on_vector), LAST)
+        w1_raw = load_passes(w1, LAST, 0, 1)
+        rounded = round_pass(w1_raw[:, 0], on_vector)
+        h = products(w1_raw[:, 0], *waiting)
+        gate_sums = open_sums(psum_gate, pass_codes(rounded), LAST)
+        hidden.append(quantise(keep, h, "_h%d" % (LAST - 1)))
         w1_raw = load_passes(w1, LAST, 1, 1)
         first_layer_pass(gate_sums, first_layer_codes(w1_raw[:, 0], on_scalar), LAST, 1)
         stationary = first_layer_codes(load_passes(w3, LAST, 0, 1)[:, 0], on_both)

@@ -2,6 +2,7 @@ from contextlib import ExitStack
 
 import concourse.mybir as mybir
 
+CFG = dict(early=4, e6='BBL', e7='BBBP', pin6=0, defer6=0, gate7=1, order=[4, 5, 6, 7], cast='SSSS', ys=[([4, 5], 'S'), ([6], 'S')], ry='SV', pf=1, prod=2, res=1)
 K, T, E, C, H, N = 1024, 1024, 8, 256, 512, 128
 R = 2
 FLOPS = 2 * E * C * (2 * K * H + H * N)
@@ -21,7 +22,7 @@ PASSES = K // K_PASS
 U = C // R
 GATHER = 2 * C
 LAST = E - 1
-LATE_W2 = 4
+LATE_W2 = CFG['early']
 FIRST_PAIR_AT = 2
 
 
@@ -33,7 +34,7 @@ def tile_moe_pke_glu_sigmoid_kernel(tc, x_words, x_scales, w1, w3, w2, offs, out
         stage = ctx.enter_context(tc.tile_pool(name="stage", bufs=8))
         code_pool = ctx.enter_context(tc.tile_pool(name="codes", bufs=12))
         slot_pool = ctx.enter_context(tc.tile_pool(name="slots", bufs=E * C // GATHER))
-        work = ctx.enter_context(tc.tile_pool(name="work", bufs=3))
+        work = ctx.enter_context(tc.tile_pool(name="work", bufs=2))
         psum_gate = ctx.enter_context(tc.psum_pool(name="psum_gate", bufs=R))
         psum_linear = ctx.enter_context(tc.psum_pool(name="psum_linear", bufs=R))
         psum_y = ctx.enter_context(tc.psum_pool(name="psum_y", bufs=4))
@@ -61,6 +62,8 @@ def tile_moe_pke_glu_sigmoid_kernel(tc, x_words, x_scales, w1, w3, w2, offs, out
         on_scalar = [nc.scalar.copy]
         on_both = [nc.vector.tensor_copy, nc.scalar.copy]
         on_vector_by_pairs = [nc.vector.tensor_copy, nc.vector.tensor_copy]
+
+        WHO = dict(V=on_vector, S=on_scalar, B=on_both, P=on_vector_by_pairs)
 
         def gather(g):
             entries = offsets[:, g * GATHER // 16 : (g + 1) * GATHER // 16]
@@ -109,12 +112,15 @@ def tile_moe_pke_glu_sigmoid_kernel(tc, x_words, x_scales, w1, w3, w2, offs, out
         def first_layer_codes(raw, copies):
             return pass_codes(round_pass(raw, copies))
 
-        def first_layer_pass(banks, stationary, e, o):
+        def first_layer_pass(banks, stationary, e, o, pairs_first=False):
             slot_words, slot_scales = all_slots[e * C // GATHER]
-            for m in range(R):
+            order = [(m, t) for m in range(R) for t in range(PACK)]
+            if pairs_first:
+                order = sorted(order, key=lambda mt: mt[1] // 2)
+            for m, t in order:
                 first = (e * C) % GATHER + m * U
                 cols = slice(first, first + U)
-                for t in range(PACK):
+                if True:
                     codes, scales = stationary[t]
                     nc.tensor.matmul_mx(
                         out=banks[m][:, t, :],
@@ -142,11 +148,11 @@ def tile_moe_pke_glu_sigmoid_kernel(tc, x_words, x_scales, w1, w3, w2, offs, out
         def gated_product(h, bank, gate):
             nc.vector.tensor_tensor(h, bank[:].rearrange("p t u -> p u t"), gate, mybir.AluOpType.mult)
 
-        def hidden_codes(e, banks, gates):
+        def hidden_values(banks, gates):
             h = work.tile([P, C, PACK], BF16, name="h", align_bytes=64)
             for m in range(R):
                 gated_product(h[:, m * U : (m + 1) * U, :], banks[m], gates[m])
-            return quantise(keep, h[:].rearrange("p c t -> p (c t)"), "_h%d" % e)
+            return h[:].rearrange("p c t -> p (c t)")
 
         def second_layer_codes(e0, count):
             raw = raw_pool.tile([P, count, PACK, N], F32, name="raw", tag="raw", align_bytes=256)
@@ -202,42 +208,106 @@ def tile_moe_pke_glu_sigmoid_kernel(tc, x_words, x_scales, w1, w3, w2, offs, out
             first_layer_pass(gate_sums, pass_codes(rounded[1]), e, 1)
             if waiting:
                 hidden.append(quantise(keep, h, "_h%d" % (e - 1)))
+            if e == LAST - 1 and CFG['e6']:
+                linear_sums = open_sums(psum_linear, first_layer_codes(load_passes(w3, e, 0, 1)[:, 0], WHO[CFG['e6'][0]]), e)
+                w3_raw = load_passes(w3, e, 1, 1)
+                first_layer_pass(linear_sums, first_layer_codes(w3_raw[:, 0], WHO[CFG['e6'][1]]), e, 1, pairs_first=True)
+                waiting = (linear_sums, sigmoids(gate_sums, w3_raw[:, 0] if CFG['e6'][2] == 'L' else w1_raw[:, 1]))
+                continue
             w3_raw = load_passes(w3, e, 0, PASSES)
             linear_sums = open_sums(psum_linear, first_layer_codes(w3_raw[:, 0], first), e)
             first_layer_pass(linear_sums, first_layer_codes(w3_raw[:, 1], on_scalar), e, 1)
             if e > 0:
                 waiting = (linear_sums, sigmoids(gate_sums, w3_raw[:, 1]))
-            if e in (2, 4):
-                second_layer_results(e - 2, second_layer_codes(e - 2, 2))
+            if e == 2:
+                second_layer_results(0, second_layer_codes(0, 2))
+            if e == 4 and LATE_W2 > 2:
+                second_layer_results(2, second_layer_codes(2, min(2, LATE_W2 - 2)))
+            if e == 5 and LATE_W2 > 4:
+                second_layer_results(4, second_layer_codes(4, 1))
 
+        late_pool = ctx.enter_context(tc.tile_pool(name="late", bufs=1))
+        ENG = dict(V=nc.vector.tensor_copy, S=nc.scalar.copy)
+
+        def load_w2(e):
+            raw = late_pool.tile([P, PACK, N], F32, name="w2_raw%d" % e, align_bytes=256)
+            nc.sync.dma_start(raw[:], w2[e].rearrange("(p j) n -> p j n", j=PACK))
+            return raw
+
+        def round_w2(raw, copy):
+            grouped = stage.tile([P, N * PACK], BF16, name="grouped", align_bytes=64)
+            copy(grouped[:].rearrange("p (c b j) -> p c j b", b=4, j=PACK), raw[:].rearrange("p j (c b) -> p c j b", b=4))
+            return grouped
+
+        def w2_codes(grouped):
+            codes, scales = quantise(code_pool, grouped[:])
+            return codes[:], scales[:]
+
+        def results(es, copy):
+            bank = psum_y.tile([P, len(es), R, U], F32, name="y", tag="y")
+            for d, e in enumerate(es):
+                second_layer_matmul(bank[:, d, :, :].rearrange("p m u -> p (m u)"), codes[e], hidden[e])
+            result = keep.tile([P, R, len(es), U], F32, name="result%d" % es[0], align_bytes=256)
+            copy(result[:].rearrange("p m e u -> p e m u"), bank[:])
+            stores.append((out_view[:, :, es[0] : es[0] + len(es), :], result))
+
+        p1, p2, p3, p4 = (WHO[x] for x in CFG['e7'])
         w1_raw = load_passes(w1, LAST, 0, 1)
-        rounded = round_pass(w1_raw[:, 0], on_vector)
-        h = products(w1_raw[:, 0], *waiting)
+        rounded = round_pass(w1_raw[:, 0], p1)
+        h6 = products(w1_raw[:, 0], *waiting) if CFG['pin6'] else hidden_values(*waiting)
         gate_sums = open_sums(psum_gate, pass_codes(rounded), LAST)
-        hidden.append(quantise(keep, h, "_h%d" % (LAST - 1)))
+        if not CFG['defer6']:
+            hidden.append(quantise(keep, h6, "_h%d" % (LAST - 1)))
         w1_raw = load_passes(w1, LAST, 1, 1)
-        first_layer_pass(gate_sums, first_layer_codes(w1_raw[:, 0], on_scalar), LAST, 1)
-        stationary = first_layer_codes(load_passes(w3, LAST, 0, 1)[:, 0], on_both)
-        gates = sigmoids(gate_sums, w1_raw[:, 0])
+        first_layer_pass(gate_sums, first_layer_codes(w1_raw[:, 0], p2), LAST, 1, pairs_first=True)
+        w3_raw = load_passes(w3, LAST, 0, 1)
+        rounded = round_pass(w3_raw[:, 0], p3)
+        gates = sigmoids(gate_sums, (w3_raw if CFG['gate7'] else w1_raw)[:, 0])
+        if CFG['defer6']:
+            pinned = [quantise(keep, g[:], "_pin%d" % k) for k, g in enumerate(rounded)]
+            groups = PACK // len(rounded)
+            stationary = [(c[:, t * P : (t + 1) * P].bitcast(FP8X4), s[:, t * P : (t + 1) * P]) for c, s in pinned for t in range(groups)]
+        else:
+            stationary = pass_codes(rounded)
         linear_sums = open_sums(psum_linear, stationary, LAST)
-        first_layer_pass(linear_sums, first_layer_codes(load_passes(w3, LAST, 1, 1)[:, 0], on_vector_by_pairs), LAST, 1)
-
-        late_codes = {e: second_layer_codes(e, 1)[0] for e in range(LATE_W2, E)}
-        for e0 in range(LATE_W2, LAST, 2):
-            second_layer_results(e0, [late_codes[e] for e in range(e0, min(e0 + 2, LAST))])
-
+        last_raw = load_passes(w3, LAST, 1, 1)[:, 0]
+        order = CFG['order']
+        raws = {e: load_w2(e) for e in order}
+        first_layer_pass(linear_sums, first_layer_codes(last_raw, p4), LAST, 1, pairs_first=CFG['pf'])
+        if CFG['defer6']:
+            hidden.append(quantise(keep, h6, "_pin0"))
+        codes = {}
         h_ranks = []
-        for m in range(R):
-            h = work.tile([P, U * PACK], BF16, name="h", align_bytes=64)
-            gated_product(h[:].rearrange("p (u t) -> p u t", t=PACK), linear_sums[m], gates[m])
-            h_ranks.append(h)
-        for m, copy in enumerate((nc.scalar.copy, nc.vector.tensor_copy)):
-            rank_codes = quantise(keep, h_ranks[m][:], "_rank%d" % m)
-            bank = psum_y.tile([P, U], F32, name="y", tag="y")
-            second_layer_matmul(bank[:], late_codes[LAST], rank_codes)
-            result = keep.tile([P, U], F32, name="rank_result%d" % m, align_bytes=256)
-            copy(result[:], bank[:])
-            stores.append((out_view[:, m, LAST, :], result))
+
+        def last_products():
+            for m in range(R):
+                h = work.tile([P, U * PACK], BF16, name="h", align_bytes=64)
+                gated_product(h[:].rearrange("p (u t) -> p u t", t=PACK), linear_sums[m], gates[m])
+                h_ranks.append(h)
+
+        def last_results():
+            for m in range(R):
+                rank_codes = quantise(keep, h_ranks[m][:], "_rank%d" % m)
+                bank = psum_y.tile([P, U], F32, name="y", tag="y")
+                second_layer_matmul(bank[:], codes[LAST], rank_codes)
+                result = keep.tile([P, U], F32, name="rank_result%d" % m, align_bytes=256)
+                ENG[CFG['ry'][m]](result[:], bank[:])
+                stores.append((out_view[:, m, LAST, :], result))
+
+        if CFG['prod'] == 0:
+            last_products()
+        for e, who in zip(order, CFG['cast']):
+            codes[e] = w2_codes(round_w2(raws[e], ENG[who]))
+        if CFG['prod'] == 1:
+            last_products()
+        if CFG['res'] == 0:
+            last_results()
+        for es, who in CFG['ys']:
+            results(es, ENG[who])
+        if CFG['prod'] == 2:
+            last_products()
+        if CFG['res'] == 1:
+            last_results()
 
         for place, result in stores:
             nc.sync.dma_start(place, result[:])

@@ -2,7 +2,6 @@ from contextlib import ExitStack
 
 import concourse.mybir as mybir
 
-CFG = dict(early=4, e6='BBL', e7='BBBP', pin6=0, defer6=0, gate7=1, order=[4, 5, 6, 7], cast='SSSS', ys=[([4, 5], 'S'), ([6], 'S')], ry='SV', pf=1, prod=2, res=1)
 K, T, E, C, H, N = 1024, 1024, 8, 256, 512, 128
 R = 2
 FLOPS = 2 * E * C * (2 * K * H + H * N)
@@ -22,8 +21,7 @@ PASSES = K // K_PASS
 U = C // R
 GATHER = 2 * C
 LAST = E - 1
-LATE_W2 = CFG['early']
-FIRST_PAIR_AT = 2
+LATE_W2 = 4
 
 
 def tile_moe_pke_glu_sigmoid_kernel(tc, x_words, x_scales, w1, w3, w2, offs, out):
@@ -51,7 +49,7 @@ def tile_moe_pke_glu_sigmoid_kernel(tc, x_words, x_scales, w1, w3, w2, offs, out
         token_scales = keep.tile([P, T // 4], I32, name="token_scales", align_bytes=256)
         nc.vector.memset(token_scales[:], 0)
         for q in range(4):
-            nc.sync.dma_start(
+            nc.scalar.dma_start(
                 token_scales[32 * q : 32 * q + 4 * PASSES, :],
                 x_scales[:, 4 * q : 4 * q + 4, :].bitcast(I32),
             )
@@ -62,8 +60,6 @@ def tile_moe_pke_glu_sigmoid_kernel(tc, x_words, x_scales, w1, w3, w2, offs, out
         on_scalar = [nc.scalar.copy]
         on_both = [nc.vector.tensor_copy, nc.scalar.copy]
         on_vector_by_pairs = [nc.vector.tensor_copy, nc.vector.tensor_copy]
-
-        WHO = dict(V=on_vector, S=on_scalar, B=on_both, P=on_vector_by_pairs)
 
         def gather(g):
             entries = offsets[:, g * GATHER // 16 : (g + 1) * GATHER // 16]
@@ -120,17 +116,16 @@ def tile_moe_pke_glu_sigmoid_kernel(tc, x_words, x_scales, w1, w3, w2, offs, out
             for m, t in order:
                 first = (e * C) % GATHER + m * U
                 cols = slice(first, first + U)
-                if True:
-                    codes, scales = stationary[t]
-                    nc.tensor.matmul_mx(
-                        out=banks[m][:, t, :],
-                        lhsT=codes,
-                        lhsT_scale=scales,
-                        rhs=slot_words[o][:, cols].bitcast(FP8X4),
-                        rhs_scale=slot_scales[4 * o :, cols],
-                        start=(o == 0 and t == 0),
-                        stop=(o == PASSES - 1 and t == PACK - 1),
-                    )
+                codes, scales = stationary[t]
+                nc.tensor.matmul_mx(
+                    out=banks[m][:, t, :],
+                    lhsT=codes,
+                    lhsT_scale=scales,
+                    rhs=slot_words[o][:, cols].bitcast(FP8X4),
+                    rhs_scale=slot_scales[4 * o :, cols],
+                    start=(o == 0 and t == 0),
+                    stop=(o == PASSES - 1 and t == PACK - 1),
+                )
 
         def open_sums(pool, stationary, e):
             banks = [pool.tile([P, PACK, U], F32, name="sums") for m in range(R)]
@@ -208,11 +203,11 @@ def tile_moe_pke_glu_sigmoid_kernel(tc, x_words, x_scales, w1, w3, w2, offs, out
             first_layer_pass(gate_sums, pass_codes(rounded[1]), e, 1)
             if waiting:
                 hidden.append(quantise(keep, h, "_h%d" % (e - 1)))
-            if e == LAST - 1 and CFG['e6']:
-                linear_sums = open_sums(psum_linear, first_layer_codes(load_passes(w3, e, 0, 1)[:, 0], WHO[CFG['e6'][0]]), e)
+            if e == LAST - 1:
+                linear_sums = open_sums(psum_linear, first_layer_codes(load_passes(w3, e, 0, 1)[:, 0], on_both), e)
                 w3_raw = load_passes(w3, e, 1, 1)
-                first_layer_pass(linear_sums, first_layer_codes(w3_raw[:, 0], WHO[CFG['e6'][1]]), e, 1, pairs_first=True)
-                waiting = (linear_sums, sigmoids(gate_sums, w3_raw[:, 0] if CFG['e6'][2] == 'L' else w1_raw[:, 1]))
+                first_layer_pass(linear_sums, first_layer_codes(w3_raw[:, 0], on_both), e, 1, pairs_first=True)
+                waiting = (linear_sums, sigmoids(gate_sums, w3_raw[:, 0]))
                 continue
             w3_raw = load_passes(w3, e, 0, PASSES)
             linear_sums = open_sums(psum_linear, first_layer_codes(w3_raw[:, 0], first), e)
@@ -221,13 +216,10 @@ def tile_moe_pke_glu_sigmoid_kernel(tc, x_words, x_scales, w1, w3, w2, offs, out
                 waiting = (linear_sums, sigmoids(gate_sums, w3_raw[:, 1]))
             if e == 2:
                 second_layer_results(0, second_layer_codes(0, 2))
-            if e == 4 and LATE_W2 > 2:
-                second_layer_results(2, second_layer_codes(2, min(2, LATE_W2 - 2)))
-            if e == 5 and LATE_W2 > 4:
-                second_layer_results(4, second_layer_codes(4, 1))
+            if e == 4:
+                second_layer_results(2, second_layer_codes(2, 2))
 
         late_pool = ctx.enter_context(tc.tile_pool(name="late", bufs=1))
-        ENG = dict(V=nc.vector.tensor_copy, S=nc.scalar.copy)
 
         def load_w2(e):
             raw = late_pool.tile([P, PACK, N], F32, name="w2_raw%d" % e, align_bytes=256)
@@ -251,63 +243,35 @@ def tile_moe_pke_glu_sigmoid_kernel(tc, x_words, x_scales, w1, w3, w2, offs, out
             copy(result[:].rearrange("p m e u -> p e m u"), bank[:])
             stores.append((out_view[:, :, es[0] : es[0] + len(es), :], result))
 
-        p1, p2, p3, p4 = (WHO[x] for x in CFG['e7'])
         w1_raw = load_passes(w1, LAST, 0, 1)
-        rounded = round_pass(w1_raw[:, 0], p1)
-        h6 = products(w1_raw[:, 0], *waiting) if CFG['pin6'] else hidden_values(*waiting)
+        rounded = round_pass(w1_raw[:, 0], on_both)
+        h = hidden_values(*waiting)
         gate_sums = open_sums(psum_gate, pass_codes(rounded), LAST)
-        if not CFG['defer6']:
-            hidden.append(quantise(keep, h6, "_h%d" % (LAST - 1)))
+        hidden.append(quantise(keep, h, "_h%d" % (LAST - 1)))
         w1_raw = load_passes(w1, LAST, 1, 1)
-        first_layer_pass(gate_sums, first_layer_codes(w1_raw[:, 0], p2), LAST, 1, pairs_first=True)
+        first_layer_pass(gate_sums, first_layer_codes(w1_raw[:, 0], on_both), LAST, 1, pairs_first=True)
         w3_raw = load_passes(w3, LAST, 0, 1)
-        rounded = round_pass(w3_raw[:, 0], p3)
-        gates = sigmoids(gate_sums, (w3_raw if CFG['gate7'] else w1_raw)[:, 0])
-        if CFG['defer6']:
-            pinned = [quantise(keep, g[:], "_pin%d" % k) for k, g in enumerate(rounded)]
-            groups = PACK // len(rounded)
-            stationary = [(c[:, t * P : (t + 1) * P].bitcast(FP8X4), s[:, t * P : (t + 1) * P]) for c, s in pinned for t in range(groups)]
-        else:
-            stationary = pass_codes(rounded)
-        linear_sums = open_sums(psum_linear, stationary, LAST)
+        rounded = round_pass(w3_raw[:, 0], on_both)
+        gates = sigmoids(gate_sums, w3_raw[:, 0])
+        linear_sums = open_sums(psum_linear, pass_codes(rounded), LAST)
         last_raw = load_passes(w3, LAST, 1, 1)[:, 0]
-        order = CFG['order']
-        raws = {e: load_w2(e) for e in order}
-        first_layer_pass(linear_sums, first_layer_codes(last_raw, p4), LAST, 1, pairs_first=CFG['pf'])
-        if CFG['defer6']:
-            hidden.append(quantise(keep, h6, "_pin0"))
-        codes = {}
+        late_raw = {e: load_w2(e) for e in range(LATE_W2, E)}
+        first_layer_pass(linear_sums, first_layer_codes(last_raw, on_vector_by_pairs), LAST, 1, pairs_first=True)
+        codes = {e: w2_codes(round_w2(late_raw[e], nc.scalar.copy)) for e in range(LATE_W2, E)}
+        results([4, 5], nc.scalar.copy)
+        results([6], nc.scalar.copy)
         h_ranks = []
-
-        def last_products():
-            for m in range(R):
-                h = work.tile([P, U * PACK], BF16, name="h", align_bytes=64)
-                gated_product(h[:].rearrange("p (u t) -> p u t", t=PACK), linear_sums[m], gates[m])
-                h_ranks.append(h)
-
-        def last_results():
-            for m in range(R):
-                rank_codes = quantise(keep, h_ranks[m][:], "_rank%d" % m)
-                bank = psum_y.tile([P, U], F32, name="y", tag="y")
-                second_layer_matmul(bank[:], codes[LAST], rank_codes)
-                result = keep.tile([P, U], F32, name="rank_result%d" % m, align_bytes=256)
-                ENG[CFG['ry'][m]](result[:], bank[:])
-                stores.append((out_view[:, m, LAST, :], result))
-
-        if CFG['prod'] == 0:
-            last_products()
-        for e, who in zip(order, CFG['cast']):
-            codes[e] = w2_codes(round_w2(raws[e], ENG[who]))
-        if CFG['prod'] == 1:
-            last_products()
-        if CFG['res'] == 0:
-            last_results()
-        for es, who in CFG['ys']:
-            results(es, ENG[who])
-        if CFG['prod'] == 2:
-            last_products()
-        if CFG['res'] == 1:
-            last_results()
+        for m in range(R):
+            h = work.tile([P, U * PACK], BF16, name="h", align_bytes=64)
+            gated_product(h[:].rearrange("p (u t) -> p u t", t=PACK), linear_sums[m], gates[m])
+            h_ranks.append(h)
+        for m, copy in enumerate([nc.scalar.copy, nc.vector.tensor_copy]):
+            rank_codes = quantise(keep, h_ranks[m][:], "_rank%d" % m)
+            bank = psum_y.tile([P, U], F32, name="y", tag="y")
+            second_layer_matmul(bank[:], codes[LAST], rank_codes)
+            result = keep.tile([P, U], F32, name="rank_result%d" % m, align_bytes=256)
+            copy(result[:], bank[:])
+            stores.append((out_view[:, m, LAST, :], result))
 
         for place, result in stores:
             nc.sync.dma_start(place, result[:])

@@ -16,25 +16,29 @@ FP8X4 = mybir.dt.float8_e4m3fn_x4
 
 P = 128
 PACK = 4
+PAIR = 2
 K_PASS = P * PACK
 PASSES = K // K_PASS
 U = C // R
 GATHER = 2 * C
 LAST = E - 1
 LATE_W2 = 4
+BY_RANKS = 5
 
 
 def tile_moe_pke_glu_sigmoid_kernel(tc, x_words, x_scales, w1, w3, w2, offs, out):
     nc = tc.nc
     with ExitStack() as ctx:
         keep = ctx.enter_context(tc.tile_pool(name="keep", bufs=1))
-        raw_pool = ctx.enter_context(tc.tile_pool(name="raw", bufs=7))
+        raw_pool = ctx.enter_context(tc.tile_pool(name="raw", bufs=6))
+        matrix_stage = ctx.enter_context(tc.tile_pool(name="matrix_stage", bufs=4))
+        matrix_code_pool = ctx.enter_context(tc.tile_pool(name="matrix_codes", bufs=3))
         stage = ctx.enter_context(tc.tile_pool(name="stage", bufs=8))
         code_pool = ctx.enter_context(tc.tile_pool(name="codes", bufs=12))
         slot_pool = ctx.enter_context(tc.tile_pool(name="slots", bufs=E * C // GATHER))
         work = ctx.enter_context(tc.tile_pool(name="work", bufs=2))
-        psum_gate = ctx.enter_context(tc.psum_pool(name="psum_gate", bufs=R))
-        psum_linear = ctx.enter_context(tc.psum_pool(name="psum_linear", bufs=R))
+        psum_gate = ctx.enter_context(tc.psum_pool(name="psum_gate", bufs=2))
+        psum_linear = ctx.enter_context(tc.psum_pool(name="psum_linear", bufs=2))
         psum_y = ctx.enter_context(tc.psum_pool(name="psum_y", bufs=4))
 
         offsets = keep.tile([P, E * C // 16], U16, name="offsets", align_bytes=256)
@@ -55,11 +59,6 @@ def tile_moe_pke_glu_sigmoid_kernel(tc, x_words, x_scales, w1, w3, w2, offs, out
             )
 
         out_view = out.rearrange("n (m e u) -> n m e u", m=R, e=E)
-
-        on_vector = [nc.vector.tensor_copy]
-        on_scalar = [nc.scalar.copy]
-        on_both = [nc.vector.tensor_copy, nc.scalar.copy]
-        on_vector_by_pairs = [nc.vector.tensor_copy, nc.vector.tensor_copy]
 
         def gather(g):
             entries = offsets[:, g * GATHER // 16 : (g + 1) * GATHER // 16]
@@ -85,85 +84,129 @@ def tile_moe_pke_glu_sigmoid_kernel(tc, x_words, x_scales, w1, w3, w2, offs, out
             nc.vector.quantize_mx(out=codes[:].bitcast(FP8X4), scales=scales[:], in_=values)
             return codes, scales
 
-        def round_pass(raw, copies):
+        def operands(codes, scales):
+            return [
+                (codes[:, n * P : (n + 1) * P].bitcast(FP8X4), scales[:, n * P : (n + 1) * P])
+                for n in range(codes.shape[1] // P)
+            ]
+
+        def round_groups(copy, grouped, raw, first, count):
             src = raw.rearrange("p j (m t) -> p m j t", t=PACK)
-            groups = PACK // len(copies)
+            copy(grouped.rearrange("p (t m j) -> p m j t", t=count, j=PACK), src[:, :, :, first : first + count])
+
+        def round_matrix(raw, copies):
+            grouped = matrix_stage.tile([P, PASSES, H * PACK], BF16, name="matrix_grouped", align_bytes=64)
+            for o, copy in enumerate(copies):
+                round_groups(copy, grouped[:, o, :], raw[:, o], 0, PACK)
+            return grouped[:].rearrange("p o c -> p (o c)")
+
+        def matrix_codes(grouped):
+            stationary = operands(*quantise(matrix_code_pool, grouped))
+            return [stationary[o * PACK : (o + 1) * PACK] for o in range(PASSES)]
+
+        def round_pairs(raw, copies):
             rounded = []
-            for n, copy in enumerate(copies):
-                grouped = stage.tile([P, groups * P * PACK], BF16, name="grouped", align_bytes=64)
-                copy(grouped[:].rearrange("p (t m j) -> p m j t", t=groups, j=PACK), src[:, :, :, n * groups : (n + 1) * groups])
+            for b, copy in enumerate(copies):
+                grouped = stage.tile([P, PAIR * P * PACK], BF16, name="grouped", align_bytes=64)
+                round_groups(copy, grouped[:], raw, b * PAIR, PAIR)
                 rounded.append(grouped)
             return rounded
 
-        def pass_codes(rounded):
-            groups = PACK // len(rounded)
+        def pair_codes(rounded):
             stationary = []
             for grouped in rounded:
-                codes, scales = quantise(code_pool, grouped[:])
-                for t in range(groups):
-                    cols = slice(t * P, (t + 1) * P)
-                    stationary.append((codes[:, cols].bitcast(FP8X4), scales[:, cols]))
+                stationary.extend(operands(*quantise(code_pool, grouped[:])))
             return stationary
 
-        def first_layer_codes(raw, copies):
-            return pass_codes(round_pass(raw, copies))
-
-        def first_layer_pass(banks, stationary, e, o, pairs_first=False):
+        def first_layer_matmul(sums, stationary, e, o, first, count, start, stop):
             slot_words, slot_scales = all_slots[e * C // GATHER]
-            order = [(m, t) for m in range(R) for t in range(PACK)]
-            if pairs_first:
-                order = sorted(order, key=lambda mt: mt[1] // 2)
-            for m, t in order:
-                first = (e * C) % GATHER + m * U
-                cols = slice(first, first + U)
-                codes, scales = stationary[t]
-                nc.tensor.matmul_mx(
-                    out=banks[m][:, t, :],
-                    lhsT=codes,
-                    lhsT_scale=scales,
-                    rhs=slot_words[o][:, cols].bitcast(FP8X4),
-                    rhs_scale=slot_scales[4 * o :, cols],
-                    start=(o == 0 and t == 0),
-                    stop=(o == PASSES - 1 and t == PACK - 1),
-                )
+            column = (e * C) % GATHER + first
+            cols = slice(column, column + count)
+            nc.tensor.matmul_mx(
+                out=sums,
+                lhsT=stationary[0],
+                lhsT_scale=stationary[1],
+                rhs=slot_words[o][:, cols].bitcast(FP8X4),
+                rhs_scale=slot_scales[4 * o :, cols],
+                start=start,
+                stop=stop,
+            )
 
-        def open_sums(pool, stationary, e):
-            banks = [pool.tile([P, PACK, U], F32, name="sums") for m in range(R)]
-            first_layer_pass(banks, stationary, e, 0)
+        def pair_banks(pool):
+            return [pool.tile([P, PAIR, C], F32, name="sums") for b in range(PACK // PAIR)]
+
+        def rank_banks(pool):
+            return [pool.tile([P, PACK, U], F32, name="sums") for m in range(R)]
+
+        def matrix_by_pairs(pool, stationary, e):
+            banks = pair_banks(pool)
+            for t in range(PACK):
+                for o in range(PASSES):
+                    first_layer_matmul(banks[t // PAIR][:, t % PAIR, :], stationary[o][t], e, o, 0, C, o == 0, o == PASSES - 1)
             return banks
 
-        def sigmoids(banks, spent):
-            gates = []
+        def matrix_by_ranks(pool, stationary, e):
+            banks = rank_banks(pool)
             for m in range(R):
-                gate = spent[:, m, :].rearrange("p (u t) -> p u t", t=PACK)
-                nc.scalar.activation(gate, banks[m][:].rearrange("p t u -> p u t"), mybir.ActivationFunctionType.Sigmoid)
-                gates.append(gate)
+                for t in range(PACK):
+                    for o in range(PASSES):
+                        first_layer_matmul(banks[m][:, t, :], stationary[o][t], e, o, m * U, U, o == 0, o == PASSES - 1)
+            return banks
+
+        def pass_by_pairs(banks, stationary, e, o):
+            for t in range(PACK):
+                start = o == 0 and t % PAIR == 0
+                stop = o == PASSES - 1 and t % PAIR == PAIR - 1
+                first_layer_matmul(banks[t // PAIR][:, t % PAIR, :], stationary[t], e, o, 0, C, start, stop)
+
+        def pass_by_ranks(banks, stationary, e, o):
+            for b in range(PACK // PAIR):
+                for m in range(R):
+                    for t in range(b * PAIR, (b + 1) * PAIR):
+                        start = o == 0 and t == 0
+                        stop = o == PASSES - 1 and t == PACK - 1
+                        first_layer_matmul(banks[m][:, t, :], stationary[t], e, o, m * U, U, start, stop)
+
+        def sigmoids(banks, spent):
+            gates = spent[:, 0:PAIR, :].rearrange("p b (c s) -> p b c s", s=PAIR)
+            for b, bank in enumerate(banks):
+                nc.scalar.activation(gates[:, b], bank[:].rearrange("p s c -> p c s"), mybir.ActivationFunctionType.Sigmoid)
             return gates
 
-        def gated_product(h, bank, gate):
-            nc.vector.tensor_tensor(h, bank[:].rearrange("p t u -> p u t"), gate, mybir.AluOpType.mult)
+        def products_by_pairs(h, banks, gates):
+            pairs = h.rearrange("p (c b s) -> p b c s", b=PACK // PAIR, s=PAIR)
+            for b, bank in enumerate(banks):
+                nc.vector.tensor_tensor(pairs[:, b], bank[:].rearrange("p s c -> p c s"), gates[:, b], mybir.AluOpType.mult)
 
-        def hidden_values(banks, gates):
-            h = work.tile([P, C, PACK], BF16, name="h", align_bytes=64)
+        def product_of_rank(h, bank, gates, m):
+            nc.vector.tensor_tensor(
+                h.rearrange("p (u b s) -> p u b s", b=PACK // PAIR, s=PAIR),
+                bank[:].rearrange("p (b s) u -> p u b s", s=PAIR),
+                gates[:, :, m * U : (m + 1) * U, :].rearrange("p b u s -> p u b s"),
+                mybir.AluOpType.mult,
+            )
+
+        def products_by_ranks(h, banks, gates):
             for m in range(R):
-                gated_product(h[:, m * U : (m + 1) * U, :], banks[m], gates[m])
-            return h[:].rearrange("p c t -> p (c t)")
+                product_of_rank(h[:, m * U * PACK : (m + 1) * U * PACK], banks[m], gates, m)
 
-        def second_layer_codes(e0, count):
-            raw = raw_pool.tile([P, count, PACK, N], F32, name="raw", tag="raw", align_bytes=256)
-            nc.sync.dma_start(raw[:], w2[e0 : e0 + count].rearrange("e (p j) n -> p e j n", j=PACK))
+        def round_w2(raw, count):
             grouped = stage.tile([P, count * N * PACK], BF16, name="grouped", align_bytes=64)
             nc.scalar.copy(
                 grouped[:].rearrange("p (d c b j) -> p d c j b", d=count, b=4, j=PACK),
-                raw[:].rearrange("p d j (c b) -> p d c j b", b=4),
+                raw.rearrange("p d j (c b) -> p d c j b", b=4),
             )
-            codes, scales = quantise(code_pool, grouped[:])
-            return [(codes[:, d * N : (d + 1) * N], scales[:, d * N : (d + 1) * N]) for d in range(count)]
+            return operands(*quantise(code_pool, grouped[:]))
+
+        def load_w2(pool, e0, count, name):
+            raw = pool.tile([P, count, PACK, N], F32, name=name, tag=name, align_bytes=256)
+            nc.sync.dma_start(raw[:], w2[e0 : e0 + count].rearrange("e (p j) n -> p e j n", j=PACK))
+            return raw
 
         def second_layer_matmul(y, stationary, moving):
             nc.tensor.matmul_mx(
                 out=y,
-                lhsT=stationary[0].bitcast(FP8X4),
+                lhsT=stationary[0],
                 lhsT_scale=stationary[1],
                 rhs=moving[0][:].bitcast(FP8X4),
                 rhs_scale=moving[1][:],
@@ -171,7 +214,7 @@ def tile_moe_pke_glu_sigmoid_kernel(tc, x_words, x_scales, w1, w3, w2, offs, out
                 stop=True,
             )
 
-        def second_layer_results(e0, w2_codes):
+        def results(e0, w2_codes):
             count = len(w2_codes)
             bank = psum_y.tile([P, count, R, U], F32, name="y", tag="y")
             for d in range(count):
@@ -180,95 +223,70 @@ def tile_moe_pke_glu_sigmoid_kernel(tc, x_words, x_scales, w1, w3, w2, offs, out
             nc.scalar.copy(result[:].rearrange("p m e u -> p e m u"), bank[:])
             stores.append((out_view[:, :, e0 : e0 + count, :], result))
 
+        vector_then_scalar = [nc.vector.tensor_copy, nc.scalar.copy]
+        scalar_alone = [nc.scalar.copy, nc.scalar.copy]
+        vector_alone = [nc.vector.tensor_copy, nc.vector.tensor_copy]
+
         hidden = []
         stores = []
         all_slots = [gather(g) for g in range(E * C // GATHER)]
 
-        def products(spent, banks, gates):
-            h = spent[:, 0, :].bitcast(BF16)
-            for m in range(R):
-                gated_product(h[:, m * U * PACK : (m + 1) * U * PACK].rearrange("p (u t) -> p u t", t=PACK), banks[m], gates[m])
-            return h
-
-        waiting = None
         for e in range(LAST):
+            copies = scalar_alone if e == 0 else vector_then_scalar
             w1_raw = load_passes(w1, e, 0, PASSES)
-            first = on_scalar if e == 0 else on_vector
-            rounded = [round_pass(w1_raw[:, 0], first), round_pass(w1_raw[:, 1], on_scalar)]
+            grouped = round_matrix(w1_raw, copies)
             if e == 1:
-                waiting = (linear_sums, sigmoids(gate_sums, w1_raw[:, 1]))
-            if waiting:
-                h = products(w1_raw[:, 0], *waiting)
-            gate_sums = open_sums(psum_gate, pass_codes(rounded[0]), e)
-            first_layer_pass(gate_sums, pass_codes(rounded[1]), e, 1)
-            if waiting:
+                gates = sigmoids(gate_sums, w1_raw[:, 1])
+            if e > 0:
+                h = w1_raw[:, 0, 0, :].bitcast(BF16)
+                products = products_by_pairs if e - 1 < BY_RANKS else products_by_ranks
+                products(h, linear_sums, gates)
+            gate_sums = matrix_by_pairs(psum_gate, matrix_codes(grouped), e)
+            if e > 0:
                 hidden.append(quantise(keep, h, "_h%d" % (e - 1)))
             if e == LAST - 1:
-                linear_sums = open_sums(psum_linear, first_layer_codes(load_passes(w3, e, 0, 1)[:, 0], on_both), e)
-                w3_raw = load_passes(w3, e, 1, 1)
-                first_layer_pass(linear_sums, first_layer_codes(w3_raw[:, 0], on_both), e, 1, pairs_first=True)
-                waiting = (linear_sums, sigmoids(gate_sums, w3_raw[:, 0]))
-                continue
+                break
             w3_raw = load_passes(w3, e, 0, PASSES)
-            linear_sums = open_sums(psum_linear, first_layer_codes(w3_raw[:, 0], first), e)
-            first_layer_pass(linear_sums, first_layer_codes(w3_raw[:, 1], on_scalar), e, 1)
+            matrix_sums = matrix_by_pairs if e < BY_RANKS else matrix_by_ranks
+            linear_sums = matrix_sums(psum_linear, matrix_codes(round_matrix(w3_raw, copies)), e)
             if e > 0:
-                waiting = (linear_sums, sigmoids(gate_sums, w3_raw[:, 1]))
-            if e == 2:
-                second_layer_results(0, second_layer_codes(0, 2))
-            if e == 4:
-                second_layer_results(2, second_layer_codes(2, 2))
+                gates = sigmoids(gate_sums, w3_raw[:, 1])
+            if e > 0 and e % 2 == 0 and e <= LATE_W2:
+                results(e - 2, round_w2(load_w2(raw_pool, e - 2, 2, "raw")[:], 2))
 
-        late_pool = ctx.enter_context(tc.tile_pool(name="late", bufs=1))
-
-        def load_w2(e):
-            raw = late_pool.tile([P, PACK, N], F32, name="w2_raw%d" % e, align_bytes=256)
-            nc.sync.dma_start(raw[:], w2[e].rearrange("(p j) n -> p j n", j=PACK))
-            return raw
-
-        def round_w2(raw, copy):
-            grouped = stage.tile([P, N * PACK], BF16, name="grouped", align_bytes=64)
-            copy(grouped[:].rearrange("p (c b j) -> p c j b", b=4, j=PACK), raw[:].rearrange("p j (c b) -> p c j b", b=4))
-            return grouped
-
-        def w2_codes(grouped):
-            codes, scales = quantise(code_pool, grouped[:])
-            return codes[:], scales[:]
-
-        def results(es, copy):
-            bank = psum_y.tile([P, len(es), R, U], F32, name="y", tag="y")
-            for d, e in enumerate(es):
-                second_layer_matmul(bank[:, d, :, :].rearrange("p m u -> p (m u)"), codes[e], hidden[e])
-            result = keep.tile([P, R, len(es), U], F32, name="result%d" % es[0], align_bytes=256)
-            copy(result[:].rearrange("p m e u -> p e m u"), bank[:])
-            stores.append((out_view[:, :, es[0] : es[0] + len(es), :], result))
-
-        w1_raw = load_passes(w1, LAST, 0, 1)
-        rounded = round_pass(w1_raw[:, 0], on_both)
-        h = hidden_values(*waiting)
-        gate_sums = open_sums(psum_gate, pass_codes(rounded), LAST)
-        hidden.append(quantise(keep, h, "_h%d" % (LAST - 1)))
-        w1_raw = load_passes(w1, LAST, 1, 1)
-        first_layer_pass(gate_sums, first_layer_codes(w1_raw[:, 0], on_both), LAST, 1, pairs_first=True)
-        w3_raw = load_passes(w3, LAST, 0, 1)
-        rounded = round_pass(w3_raw[:, 0], on_both)
+        linear_sums = rank_banks(psum_linear)
+        for o in range(PASSES):
+            w3_raw = load_passes(w3, LAST - 1, o, 1)
+            pass_by_ranks(linear_sums, pair_codes(round_pairs(w3_raw[:, 0], vector_then_scalar)), LAST - 1, o)
         gates = sigmoids(gate_sums, w3_raw[:, 0])
-        linear_sums = open_sums(psum_linear, pass_codes(rounded), LAST)
-        last_raw = load_passes(w3, LAST, 1, 1)[:, 0]
-        late_raw = {e: load_w2(e) for e in range(LATE_W2, E)}
-        first_layer_pass(linear_sums, first_layer_codes(last_raw, on_vector_by_pairs), LAST, 1, pairs_first=True)
-        codes = {e: w2_codes(round_w2(late_raw[e], nc.scalar.copy)) for e in range(LATE_W2, E)}
-        results([4, 5], nc.scalar.copy)
-        results([6], nc.scalar.copy)
+
+        rounded = round_pairs(load_passes(w1, LAST, 0, 1)[:, 0], vector_then_scalar)
+        h = work.tile([P, C * PACK], BF16, name="h", align_bytes=64)
+        products_by_ranks(h[:], linear_sums, gates)
+        gate_sums = pair_banks(psum_gate)
+        pass_by_pairs(gate_sums, pair_codes(rounded), LAST, 0)
+        hidden.append(quantise(keep, h[:], "_h%d" % (LAST - 1)))
+        pass_by_pairs(gate_sums, pair_codes(round_pairs(load_passes(w1, LAST, 1, 1)[:, 0], vector_then_scalar)), LAST, 1)
+        w3_raw = load_passes(w3, LAST, 0, 1)
+        rounded = round_pairs(w3_raw[:, 0], vector_then_scalar)
+        gates = sigmoids(gate_sums, w3_raw[:, 0])
+        linear_sums = rank_banks(psum_linear)
+        pass_by_ranks(linear_sums, pair_codes(rounded), LAST, 0)
+        last_raw = load_passes(w3, LAST, 1, 1)
+        late_raw = [load_w2(keep, e, 1, "w2_raw%d" % e) for e in range(LATE_W2, E)]
+        pass_by_ranks(linear_sums, pair_codes(round_pairs(last_raw[:, 0], vector_alone)), LAST, 1)
+        late_codes = [round_w2(raw[:], 1)[0] for raw in late_raw]
+        results(LATE_W2, late_codes[0:2])
+        results(LATE_W2 + 2, late_codes[2:3])
         h_ranks = []
         for m in range(R):
             h = work.tile([P, U * PACK], BF16, name="h", align_bytes=64)
-            gated_product(h[:].rearrange("p (u t) -> p u t", t=PACK), linear_sums[m], gates[m])
+            product_of_rank(h[:], linear_sums[m], gates, m)
             h_ranks.append(h)
         for m, copy in enumerate([nc.scalar.copy, nc.vector.tensor_copy]):
             rank_codes = quantise(keep, h_ranks[m][:], "_rank%d" % m)
             bank = psum_y.tile([P, U], F32, name="y", tag="y")
-            second_layer_matmul(bank[:], codes[LAST], rank_codes)
+            second_layer_matmul(bank[:], late_codes[-1], rank_codes)
             result = keep.tile([P, U], F32, name="rank_result%d" % m, align_bytes=256)
             copy(result[:], bank[:])
             stores.append((out_view[:, m, LAST, :], result))

@@ -221,7 +221,11 @@ def tile_moe_pke_glu_sigmoid_kernel(tc, x_words, x_scales, w1, w3, w2, offs, out
                 second_layer_matmul(bank[:, d, :, :].rearrange("p m u -> p (m u)"), w2_codes[d], hidden[e0 + d])
             result = keep.tile([P, R, count, U], F32, name="result%d" % e0, align_bytes=256)
             nc.scalar.copy(result[:].rearrange("p m e u -> p e m u"), bank[:])
-            stores.append((out_view[:, :, e0 : e0 + count, :], result))
+            if e0 < LATE_W2:
+                for m in range(R):
+                    stores.append((out_view[:, m, e0 : e0 + count, :], result[:, m]))
+            else:
+                stores.append((out_view[:, :, e0 : e0 + count, :], result[:]))
 
         vector_then_scalar = [nc.vector.tensor_copy, nc.scalar.copy]
         scalar_alone = [nc.scalar.copy, nc.scalar.copy]
@@ -257,7 +261,8 @@ def tile_moe_pke_glu_sigmoid_kernel(tc, x_words, x_scales, w1, w3, w2, offs, out
         linear_sums = rank_banks(psum_linear)
         for o in range(PASSES):
             w3_raw = load_passes(w3, LAST - 1, o, 1)
-            pass_by_ranks(linear_sums, pair_codes(round_pairs(w3_raw[:, 0], vector_then_scalar)), LAST - 1, o)
+            copies = scalar_alone if o == 0 else vector_then_scalar
+            pass_by_ranks(linear_sums, pair_codes(round_pairs(w3_raw[:, 0], copies)), LAST - 1, o)
         gates = sigmoids(gate_sums, w3_raw[:, 0])
 
         rounded = round_pairs(load_passes(w1, LAST, 0, 1)[:, 0], vector_then_scalar)
@@ -266,12 +271,14 @@ def tile_moe_pke_glu_sigmoid_kernel(tc, x_words, x_scales, w1, w3, w2, offs, out
         gate_sums = pair_banks(psum_gate)
         pass_by_pairs(gate_sums, pair_codes(rounded), LAST, 0)
         hidden.append(quantise(keep, h[:], "_h%d" % (LAST - 1)))
-        pass_by_pairs(gate_sums, pair_codes(round_pairs(load_passes(w1, LAST, 1, 1)[:, 0], vector_then_scalar)), LAST, 1)
+        second = pair_codes(round_pairs(load_passes(w1, LAST, 1, 1)[:, 0], vector_then_scalar))
+        pass_by_pairs(gate_sums, second, LAST, 1)
         w3_raw = load_passes(w3, LAST, 0, 1)
         rounded = round_pairs(w3_raw[:, 0], vector_then_scalar)
         gates = sigmoids(gate_sums, w3_raw[:, 0])
         linear_sums = rank_banks(psum_linear)
-        pass_by_ranks(linear_sums, pair_codes(rounded), LAST, 0)
+        third = pair_codes(rounded)
+        pass_by_ranks(linear_sums, third, LAST, 0)
         last_raw = load_passes(w3, LAST, 1, 1)
         late_raw = [load_w2(keep, e, 1, "w2_raw%d" % e) for e in range(LATE_W2, E)]
         pass_by_ranks(linear_sums, pair_codes(round_pairs(last_raw[:, 0], vector_alone)), LAST, 1)
@@ -289,7 +296,7 @@ def tile_moe_pke_glu_sigmoid_kernel(tc, x_words, x_scales, w1, w3, w2, offs, out
             second_layer_matmul(bank[:], late_codes[-1], rank_codes)
             result = keep.tile([P, U], F32, name="rank_result%d" % m, align_bytes=256)
             copy(result[:], bank[:])
-            stores.append((out_view[:, m, LAST, :], result))
+            stores.append((out_view[:, m, LAST, :], result[:]))
 
         for place, result in stores:
-            nc.sync.dma_start(place, result[:])
+            nc.sync.dma_start(place, result)

@@ -31,8 +31,8 @@ def tile_moe_pke_glu_sigmoid_kernel(tc, x_words, x_scales, w1, w3, w2, offs, out
     with ExitStack() as ctx:
         keep = ctx.enter_context(tc.tile_pool(name="keep", bufs=1))
         raw_pool = ctx.enter_context(tc.tile_pool(name="raw", bufs=6))
-        matrix_stage = ctx.enter_context(tc.tile_pool(name="matrix_stage", bufs=4))
-        matrix_code_pool = ctx.enter_context(tc.tile_pool(name="matrix_codes", bufs=3))
+        matrix_stage = ctx.enter_context(tc.tile_pool(name="matrix_stage", bufs=8))
+        matrix_code_pool = ctx.enter_context(tc.tile_pool(name="matrix_codes", bufs=6))
         stage = ctx.enter_context(tc.tile_pool(name="stage", bufs=8))
         code_pool = ctx.enter_context(tc.tile_pool(name="codes", bufs=12))
         slot_pool = ctx.enter_context(tc.tile_pool(name="slots", bufs=E * C // GATHER))
@@ -52,11 +52,10 @@ def tile_moe_pke_glu_sigmoid_kernel(tc, x_words, x_scales, w1, w3, w2, offs, out
 
         token_scales = keep.tile([P, T // 4], I32, name="token_scales", align_bytes=256)
         nc.vector.memset(token_scales[:], 0)
-        for q in range(4):
-            nc.scalar.dma_start(
-                token_scales[32 * q : 32 * q + 4 * PASSES, :],
-                x_scales[:, 4 * q : 4 * q + 4, :].bitcast(I32),
-            )
+
+        def load_scale_rows(o):
+            for r in range(4):
+                nc.scalar.dma_start(token_scales[4 * o + r : P : 32, :], x_scales[o, r:16:4, :].bitcast(I32))
 
         out_view = out.rearrange("n (m e u) -> n m e u", m=R, e=E)
 
@@ -95,14 +94,17 @@ def tile_moe_pke_glu_sigmoid_kernel(tc, x_words, x_scales, w1, w3, w2, offs, out
             copy(grouped.rearrange("p (t m j) -> p m j t", t=count, j=PACK), src[:, :, :, first : first + count])
 
         def round_matrix(raw, copies):
-            grouped = matrix_stage.tile([P, PASSES, H * PACK], BF16, name="matrix_grouped", align_bytes=64)
+            rounded = []
             for o, copy in enumerate(copies):
-                round_groups(copy, grouped[:, o, :], raw[:, o], 0, PACK)
-            return grouped[:].rearrange("p o c -> p (o c)")
+                grouped = matrix_stage.tile([P, H * PACK], BF16, name="matrix_grouped", align_bytes=64)
+                round_groups(copy, grouped[:], raw[:, o], 0, PACK)
+                rounded.append(grouped)
+            return rounded
 
-        def matrix_codes(grouped):
-            stationary = operands(*quantise(matrix_code_pool, grouped))
-            return [stationary[o * PACK : (o + 1) * PACK] for o in range(PASSES)]
+        def matrix_sums(banks, one_pass, rounded, e):
+            for o, grouped in enumerate(rounded):
+                one_pass(banks, operands(*quantise(matrix_code_pool, grouped[:])), e, o)
+            return banks
 
         def round_pairs(raw, copies):
             rounded = []
@@ -137,21 +139,6 @@ def tile_moe_pke_glu_sigmoid_kernel(tc, x_words, x_scales, w1, w3, w2, offs, out
 
         def rank_banks(pool):
             return [pool.tile([P, PACK, U], F32, name="sums") for m in range(R)]
-
-        def matrix_by_pairs(pool, stationary, e):
-            banks = pair_banks(pool)
-            for t in range(PACK):
-                for o in range(PASSES):
-                    first_layer_matmul(banks[t // PAIR][:, t % PAIR, :], stationary[o][t], e, o, 0, C, o == 0, o == PASSES - 1)
-            return banks
-
-        def matrix_by_ranks(pool, stationary, e):
-            banks = rank_banks(pool)
-            for m in range(R):
-                for t in range(PACK):
-                    for o in range(PASSES):
-                        first_layer_matmul(banks[m][:, t, :], stationary[o][t], e, o, m * U, U, o == 0, o == PASSES - 1)
-            return banks
 
         def pass_by_pairs(banks, stationary, e, o):
             for t in range(PACK):
@@ -190,13 +177,13 @@ def tile_moe_pke_glu_sigmoid_kernel(tc, x_words, x_scales, w1, w3, w2, offs, out
             for m in range(R):
                 product_of_rank(h[:, m * U * PACK : (m + 1) * U * PACK], banks[m], gates, m)
 
-        def round_w2(raw, count):
-            grouped = stage.tile([P, count * N * PACK], BF16, name="grouped", align_bytes=64)
+        def round_w2(raw, count, stage_pool, codes_pool, name):
+            grouped = stage_pool.tile([P, count * N * PACK], BF16, name=name, align_bytes=64)
             nc.scalar.copy(
                 grouped[:].rearrange("p (d c b j) -> p d c j b", d=count, b=4, j=PACK),
                 raw.rearrange("p d j (c b) -> p d c j b", b=4),
             )
-            return operands(*quantise(code_pool, grouped[:]))
+            return operands(*quantise(codes_pool, grouped[:]))
 
         def load_w2(pool, e0, count, name):
             raw = pool.tile([P, count, PACK, N], F32, name=name, tag=name, align_bytes=256)
@@ -214,18 +201,16 @@ def tile_moe_pke_glu_sigmoid_kernel(tc, x_words, x_scales, w1, w3, w2, offs, out
                 stop=True,
             )
 
-        def results(e0, w2_codes):
-            count = len(w2_codes)
-            bank = psum_y.tile([P, count, R, U], F32, name="y", tag="y")
-            for d in range(count):
-                second_layer_matmul(bank[:, d, :, :].rearrange("p m u -> p (m u)"), w2_codes[d], hidden[e0 + d])
-            result = keep.tile([P, R, count, U], F32, name="result%d" % e0, align_bytes=256)
-            nc.scalar.copy(result[:].rearrange("p m e u -> p e m u"), bank[:])
-            if e0 < LATE_W2:
-                for m in range(R):
-                    stores.append((out_view[:, m, e0 : e0 + count, :], result[:, m]))
-            else:
-                stores.append((out_view[:, :, e0 : e0 + count, :], result[:]))
+        def results(e0, w2_codes, result):
+            bank = psum_y.tile([P, len(w2_codes), R, U], F32, name="y", tag="y")
+            for d, stationary in enumerate(w2_codes):
+                second_layer_matmul(bank[:, d, :, :].rearrange("p m u -> p (m u)"), stationary, hidden[e0 + d])
+            nc.scalar.copy(result.rearrange("p m e u -> p e m u"), bank[:])
+
+        def late_results(e0, w2_codes):
+            result = keep.tile([P, R, len(w2_codes), U], F32, name="result%d" % e0, align_bytes=256)
+            results(e0, w2_codes, result[:])
+            stores.append((out_view[:, :, e0 : e0 + len(w2_codes), :], result[:]))
 
         vector_then_scalar = [nc.vector.tensor_copy, nc.scalar.copy]
         scalar_alone = [nc.scalar.copy, nc.scalar.copy]
@@ -233,11 +218,14 @@ def tile_moe_pke_glu_sigmoid_kernel(tc, x_words, x_scales, w1, w3, w2, offs, out
 
         hidden = []
         stores = []
+        load_scale_rows(0)
+        first_raw = load_passes(w1, 0, 0, PASSES)
+        load_scale_rows(1)
         all_slots = [gather(g) for g in range(E * C // GATHER)]
 
         for e in range(LAST):
             copies = scalar_alone if e == 0 else vector_then_scalar
-            w1_raw = load_passes(w1, e, 0, PASSES)
+            w1_raw = first_raw if e == 0 else load_passes(w1, e, 0, PASSES)
             grouped = round_matrix(w1_raw, copies)
             if e == 1:
                 gates = sigmoids(gate_sums, w1_raw[:, 1])
@@ -245,18 +233,24 @@ def tile_moe_pke_glu_sigmoid_kernel(tc, x_words, x_scales, w1, w3, w2, offs, out
                 h = w1_raw[:, 0, 0, :].bitcast(BF16)
                 products = products_by_pairs if e - 1 < BY_RANKS else products_by_ranks
                 products(h, linear_sums, gates)
-            gate_sums = matrix_by_pairs(psum_gate, matrix_codes(grouped), e)
+            gate_sums = matrix_sums(pair_banks(psum_gate), pass_by_pairs, grouped, e)
             if e > 0:
                 hidden.append(quantise(keep, h, "_h%d" % (e - 1)))
             if e == LAST - 1:
                 break
             w3_raw = load_passes(w3, e, 0, PASSES)
-            matrix_sums = matrix_by_pairs if e < BY_RANKS else matrix_by_ranks
-            linear_sums = matrix_sums(psum_linear, matrix_codes(round_matrix(w3_raw, copies)), e)
+            banks, one_pass = (pair_banks, pass_by_pairs) if e < BY_RANKS else (rank_banks, pass_by_ranks)
+            linear_sums = matrix_sums(banks(psum_linear), one_pass, round_matrix(w3_raw, copies), e)
             if e > 0:
                 gates = sigmoids(gate_sums, w3_raw[:, 1])
-            if e > 0 and e % 2 == 0 and e <= LATE_W2:
-                results(e - 2, round_w2(load_w2(raw_pool, e - 2, 2, "raw")[:], 2))
+            if e == LATE_W2 - 1:
+                early_raw = load_w2(raw_pool, 0, LATE_W2, "raw")
+                early_codes = round_w2(early_raw[:], LATE_W2, matrix_stage, matrix_code_pool, "matrix_grouped")
+            if e == LATE_W2 + 1:
+                result = w1_raw[:, 1, 0:R, :].rearrange("p m (e u) -> p m e u", u=U)
+                for e0 in range(0, LATE_W2, 2):
+                    results(e0, early_codes[e0 : e0 + 2], result[:, :, e0 : e0 + 2, :])
+                stores.append((out_view[:, :, 0:LATE_W2, :], result))
 
         linear_sums = rank_banks(psum_linear)
         for o in range(PASSES):
@@ -282,9 +276,9 @@ def tile_moe_pke_glu_sigmoid_kernel(tc, x_words, x_scales, w1, w3, w2, offs, out
         last_raw = load_passes(w3, LAST, 1, 1)
         late_raw = [load_w2(keep, e, 1, "w2_raw%d" % e) for e in range(LATE_W2, E)]
         pass_by_ranks(linear_sums, pair_codes(round_pairs(last_raw[:, 0], vector_alone)), LAST, 1)
-        late_codes = [round_w2(raw[:], 1)[0] for raw in late_raw]
-        results(LATE_W2, late_codes[0:2])
-        results(LATE_W2 + 2, late_codes[2:3])
+        late_codes = [round_w2(raw[:], 1, stage, code_pool, "grouped")[0] for raw in late_raw]
+        late_results(LATE_W2, late_codes[0:2])
+        late_results(LATE_W2 + 2, late_codes[2:3])
         h_ranks = []
         for m in range(R):
             h = work.tile([P, U * PACK], BF16, name="h", align_bytes=64)

@@ -29,11 +29,12 @@ BY_RANKS = 5
 def tile_moe_pke_glu_sigmoid_kernel(tc, x_words, x_scales, w1, w3, w2, offs, out):
     nc = tc.nc
     with ExitStack() as ctx:
-        keep = ctx.enter_context(tc.tile_pool(name="keep", bufs=1))
         raw_pool = ctx.enter_context(tc.tile_pool(name="raw", bufs=6))
-        matrix_stage = ctx.enter_context(tc.tile_pool(name="matrix_stage", bufs=8))
+        token_pool = ctx.enter_context(tc.tile_pool(name="tokens", bufs=1))
+        keep = ctx.enter_context(tc.tile_pool(name="keep", bufs=1))
+        matrix_stage = ctx.enter_context(tc.tile_pool(name="matrix_stage", bufs=6))
         matrix_code_pool = ctx.enter_context(tc.tile_pool(name="matrix_codes", bufs=6))
-        stage = ctx.enter_context(tc.tile_pool(name="stage", bufs=8))
+        stage = ctx.enter_context(tc.tile_pool(name="stage", bufs=7))
         code_pool = ctx.enter_context(tc.tile_pool(name="codes", bufs=12))
         slot_pool = ctx.enter_context(tc.tile_pool(name="slots", bufs=E * C // GATHER))
         work = ctx.enter_context(tc.tile_pool(name="work", bufs=2))
@@ -46,7 +47,7 @@ def tile_moe_pke_glu_sigmoid_kernel(tc, x_words, x_scales, w1, w3, w2, offs, out
 
         token_words = []
         for o in range(PASSES):
-            words = keep.tile([P, T], I32, name="token_words%d" % o, align_bytes=256)
+            words = token_pool.tile([P, T], I32, name="token_words%d" % o, align_bytes=4096)
             nc.sync.dma_start(words[:], x_words[o].rearrange("p t r -> p (t r)").bitcast(I32))
             token_words.append(words)
 
@@ -71,7 +72,7 @@ def tile_moe_pke_glu_sigmoid_kernel(tc, x_words, x_scales, w1, w3, w2, offs, out
             return slot_words, slot_scales
 
         def load_passes(w, e, first, count):
-            raw = raw_pool.tile([P, count, PACK, H], F32, name="raw", tag="raw", align_bytes=256)
+            raw = raw_pool.tile([P, count, PACK, H], F32, name="raw", tag="raw", align_bytes=4096)
             rows = w[e, first * K_PASS : (first + count) * K_PASS, :]
             nc.sync.dma_start(raw[:], rows.rearrange("(o p j) c -> p o j c", p=P, j=PACK))
             return raw
@@ -185,8 +186,8 @@ def tile_moe_pke_glu_sigmoid_kernel(tc, x_words, x_scales, w1, w3, w2, offs, out
             )
             return operands(*quantise(codes_pool, grouped[:]))
 
-        def load_w2(pool, e0, count, name):
-            raw = pool.tile([P, count, PACK, N], F32, name=name, tag=name, align_bytes=256)
+        def load_w2(pool, e0, count, name, align):
+            raw = pool.tile([P, count, PACK, N], F32, name=name, tag=name, align_bytes=align)
             nc.sync.dma_start(raw[:], w2[e0 : e0 + count].rearrange("e (p j) n -> p e j n", j=PACK))
             return raw
 
@@ -244,7 +245,7 @@ def tile_moe_pke_glu_sigmoid_kernel(tc, x_words, x_scales, w1, w3, w2, offs, out
             if e > 0:
                 gates = sigmoids(gate_sums, w3_raw[:, 1])
             if e == LATE_W2 - 1:
-                early_raw = load_w2(raw_pool, 0, LATE_W2, "raw")
+                early_raw = load_w2(raw_pool, 0, LATE_W2, "raw", 4096)
                 early_codes = round_w2(early_raw[:], LATE_W2, matrix_stage, matrix_code_pool, "matrix_grouped")
             if e == LATE_W2 + 1:
                 result = w1_raw[:, 1, 0:R, :].rearrange("p m (e u) -> p m e u", u=U)
@@ -274,7 +275,7 @@ def tile_moe_pke_glu_sigmoid_kernel(tc, x_words, x_scales, w1, w3, w2, offs, out
         third = pair_codes(rounded)
         pass_by_ranks(linear_sums, third, LAST, 0)
         last_raw = load_passes(w3, LAST, 1, 1)
-        late_raw = [load_w2(keep, e, 1, "w2_raw%d" % e) for e in range(LATE_W2, E)]
+        late_raw = [load_w2(token_pool, e, 1, "w2_raw%d" % e, 2048) for e in range(LATE_W2, E)]
         pass_by_ranks(linear_sums, pair_codes(round_pairs(last_raw[:, 0], vector_alone)), LAST, 1)
         late_codes = [round_w2(raw[:], 1, stage, code_pool, "grouped")[0] for raw in late_raw]
         late_results(LATE_W2, late_codes[0:2])

from contextlib import ExitStack

import concourse.mybir as mybir

K, T, E, C, H, N = 1024, 1024, 8, 256, 512, 128
R = 2
FLOPS = 2 * E * C * (2 * K * H + H * N)

F32 = mybir.dt.float32
BF16 = mybir.dt.bfloat16
I32 = mybir.dt.int32
U32 = mybir.dt.uint32
U16 = mybir.dt.uint16
U8 = mybir.dt.uint8
FP8X4 = mybir.dt.float8_e4m3fn_x4

P = 128
PACK = 4
PAIR = 2
K_PASS = P * PACK
PASSES = K // K_PASS
U = C // R
GATHER = 2 * C
LAST = E - 1
LATE_W2 = 4
BY_RANKS = 5


def tile_moe_pke_glu_sigmoid_kernel(tc, x_words, x_scales, w1, w3, w2, offs, out):
    nc = tc.nc
    with ExitStack() as ctx:
        raw_pool = ctx.enter_context(tc.tile_pool(name="raw", bufs=6))
        token_pool = ctx.enter_context(tc.tile_pool(name="tokens", bufs=1))
        keep = ctx.enter_context(tc.tile_pool(name="keep", bufs=1))
        matrix_stage = ctx.enter_context(tc.tile_pool(name="matrix_stage", bufs=6))
        matrix_code_pool = ctx.enter_context(tc.tile_pool(name="matrix_codes", bufs=6))
        stage = ctx.enter_context(tc.tile_pool(name="stage", bufs=7))
        code_pool = ctx.enter_context(tc.tile_pool(name="codes", bufs=12))
        slot_pool = ctx.enter_context(tc.tile_pool(name="slots", bufs=E * C // GATHER))
        work = ctx.enter_context(tc.tile_pool(name="work", bufs=2))
        psum_gate = ctx.enter_context(tc.psum_pool(name="psum_gate", bufs=2))
        psum_linear = ctx.enter_context(tc.psum_pool(name="psum_linear", bufs=2))
        psum_y = ctx.enter_context(tc.psum_pool(name="psum_y", bufs=4))

        offsets = keep.tile([P, E * C // 16], U16, name="offsets", align_bytes=256)
        nc.sync.dma_start(offsets[:], offs)

        token_words = []
        for o in range(PASSES):
            words = token_pool.tile([P, T], I32, name="token_words%d" % o, align_bytes=4096)
            nc.sync.dma_start(words[:], x_words[o].rearrange("p t r -> p (t r)").bitcast(I32))
            token_words.append(words)

        token_scales = keep.tile([P, T // 4], I32, name="token_scales", align_bytes=256)
        nc.vector.memset(token_scales[:], 0)

        def load_scale_rows(o):
            for r in range(4):
                nc.scalar.dma_start(token_scales[4 * o + r : P : 32, :], x_scales[o, r:16:4, :].bitcast(I32))

        out_view = out.rearrange("n (m e u) -> n m e u", m=R, e=E)

        def gather(g):
            entries = offsets[:, g * GATHER // 16 : (g + 1) * GATHER // 16]
            slot_words = []
            for o in range(PASSES):
                words = slot_pool.tile([P, GATHER], U32, name="slot_words%d" % o, align_bytes=64)
                nc.vector.tensor_copy(words[:], token_words[o][:].bitcast(U32).indirect(entries))
                slot_words.append(words)
            slot_scales = slot_pool.tile([P, GATHER], U8, name="slot_scales", align_bytes=64)
            nc.vector.tensor_copy(slot_scales[:], token_scales[:].bitcast(U8).indirect(entries))
            return slot_words, slot_scales

        def load_passes(w, e, first, count):
            raw = raw_pool.tile([P, count, PACK, H], F32, name="raw", tag="raw", align_bytes=4096)
            rows = w[e, first * K_PASS : (first + count) * K_PASS, :]
            nc.sync.dma_start(raw[:], rows.rearrange("(o p j) c -> p o j c", p=P, j=PACK))
            return raw

        def quantise(pool, values, tag=""):
            columns = values.shape[1] // PACK
            codes = pool.tile([P, columns], U32, name="codes" + tag, align_bytes=64)
            scales = pool.tile([P, columns], U8, name="scales" + tag, align_bytes=64)
            nc.vector.quantize_mx(out=codes[:].bitcast(FP8X4), scales=scales[:], in_=values)
            return codes, scales

        def operands(codes, scales):
            return [
                (codes[:, n * P : (n + 1) * P].bitcast(FP8X4), scales[:, n * P : (n + 1) * P])
                for n in range(codes.shape[1] // P)
            ]

        def round_groups(copy, grouped, raw, first, count):
            src = raw.rearrange("p j (m t) -> p m j t", t=PACK)
            copy(grouped.rearrange("p (t m j) -> p m j t", t=count, j=PACK), src[:, :, :, first : first + count])

        def round_matrix(raw, copies):
            rounded = []
            for o, copy in enumerate(copies):
                grouped = matrix_stage.tile([P, H * PACK], BF16, name="matrix_grouped", align_bytes=64)
                round_groups(copy, grouped[:], raw[:, o], 0, PACK)
                rounded.append(grouped)
            return rounded

        def matrix_sums(banks, one_pass, rounded, e):
            for o, grouped in enumerate(rounded):
                one_pass(banks, operands(*quantise(matrix_code_pool, grouped[:])), e, o)
            return banks

        def round_pairs(raw, copies):
            rounded = []
            for b, copy in enumerate(copies):
                grouped = stage.tile([P, PAIR * P * PACK], BF16, name="grouped", align_bytes=64)
                round_groups(copy, grouped[:], raw, b * PAIR, PAIR)
                rounded.append(grouped)
            return rounded

        def pair_codes(rounded):
            stationary = []
            for grouped in rounded:
                stationary.extend(operands(*quantise(code_pool, grouped[:])))
            return stationary

        def first_layer_matmul(sums, stationary, e, o, first, count, start, stop):
            slot_words, slot_scales = all_slots[e * C // GATHER]
            column = (e * C) % GATHER + first
            cols = slice(column, column + count)
            nc.tensor.matmul_mx(
                out=sums,
                lhsT=stationary[0],
                lhsT_scale=stationary[1],
                rhs=slot_words[o][:, cols].bitcast(FP8X4),
                rhs_scale=slot_scales[4 * o :, cols],
                start=start,
                stop=stop,
            )

        def pair_banks(pool):
            return [pool.tile([P, PAIR, C], F32, name="sums") for b in range(PACK // PAIR)]

        def rank_banks(pool):
            return [pool.tile([P, PACK, U], F32, name="sums") for m in range(R)]

        def pass_by_pairs(banks, stationary, e, o):
            for t in range(PACK):
                start = o == 0 and t % PAIR == 0
                stop = o == PASSES - 1 and t % PAIR == PAIR - 1
                first_layer_matmul(banks[t // PAIR][:, t % PAIR, :], stationary[t], e, o, 0, C, start, stop)

        def pass_by_ranks(banks, stationary, e, o):
            for b in range(PACK // PAIR):
                for m in range(R):
                    for t in range(b * PAIR, (b + 1) * PAIR):
                        start = o == 0 and t == 0
                        stop = o == PASSES - 1 and t == PACK - 1
                        first_layer_matmul(banks[m][:, t, :], stationary[t], e, o, m * U, U, start, stop)

        def sigmoids(banks, spent):
            gates = spent[:, 0:PAIR, :].rearrange("p b (c s) -> p b c s", s=PAIR)
            for b, bank in enumerate(banks):
                nc.scalar.activation(gates[:, b], bank[:].rearrange("p s c -> p c s"), mybir.ActivationFunctionType.Sigmoid)
            return gates

        def products_by_pairs(h, banks, gates):
            pairs = h.rearrange("p (c b s) -> p b c s", b=PACK // PAIR, s=PAIR)
            for b, bank in enumerate(banks):
                nc.vector.tensor_tensor(pairs[:, b], bank[:].rearrange("p s c -> p c s"), gates[:, b], mybir.AluOpType.mult)

        def product_of_rank(h, bank, gates, m):
            nc.vector.tensor_tensor(
                h.rearrange("p (u b s) -> p u b s", b=PACK // PAIR, s=PAIR),
                bank[:].rearrange("p (b s) u -> p u b s", s=PAIR),
                gates[:, :, m * U : (m + 1) * U, :].rearrange("p b u s -> p u b s"),
                mybir.AluOpType.mult,
            )

        def products_by_ranks(h, banks, gates):
            for m in range(R):
                product_of_rank(h[:, m * U * PACK : (m + 1) * U * PACK], banks[m], gates, m)

        def round_w2(raw, count, stage_pool, codes_pool, name):
            grouped = stage_pool.tile([P, count * N * PACK], BF16, name=name, align_bytes=64)
            nc.scalar.copy(
                grouped[:].rearrange("p (d c b j) -> p d c j b", d=count, b=4, j=PACK),
                raw.rearrange("p d j (c b) -> p d c j b", b=4),
            )
            return operands(*quantise(codes_pool, grouped[:]))

        def load_w2(pool, e0, count, name, align):
            raw = pool.tile([P, count, PACK, N], F32, name=name, tag=name, align_bytes=align)
            nc.sync.dma_start(raw[:], w2[e0 : e0 + count].rearrange("e (p j) n -> p e j n", j=PACK))
            return raw

        def second_layer_matmul(y, stationary, moving):
            nc.tensor.matmul_mx(
                out=y,
                lhsT=stationary[0],
                lhsT_scale=stationary[1],
                rhs=moving[0][:].bitcast(FP8X4),
                rhs_scale=moving[1][:],
                start=True,
                stop=True,
            )

        def results(e0, w2_codes, result):
            bank = psum_y.tile([P, len(w2_codes), R, U], F32, name="y", tag="y")
            for d, stationary in enumerate(w2_codes):
                second_layer_matmul(bank[:, d, :, :].rearrange("p m u -> p (m u)"), stationary, hidden[e0 + d])
            nc.scalar.copy(result.rearrange("p m e u -> p e m u"), bank[:])

        def late_results(e0, w2_codes):
            result = keep.tile([P, R, len(w2_codes), U], F32, name="result%d" % e0, align_bytes=256)
            results(e0, w2_codes, result[:])
            stores.append((out_view[:, :, e0 : e0 + len(w2_codes), :], result[:]))

        vector_then_scalar = [nc.vector.tensor_copy, nc.scalar.copy]
        scalar_alone = [nc.scalar.copy, nc.scalar.copy]
        vector_alone = [nc.vector.tensor_copy, nc.vector.tensor_copy]

        hidden = []
        stores = []
        load_scale_rows(0)
        first_raw = load_passes(w1, 0, 0, PASSES)
        load_scale_rows(1)
        all_slots = [gather(g) for g in range(E * C // GATHER)]

        for e in range(LAST):
            copies = scalar_alone if e == 0 else vector_then_scalar
            w1_raw = first_raw if e == 0 else load_passes(w1, e, 0, PASSES)
            grouped = round_matrix(w1_raw, copies)
            if e == 1:
                gates = sigmoids(gate_sums, w1_raw[:, 1])
            if e > 0:
                h = w1_raw[:, 0, 0, :].bitcast(BF16)
                products = products_by_pairs if e - 1 < BY_RANKS else products_by_ranks
                products(h, linear_sums, gates)
            gate_sums = matrix_sums(pair_banks(psum_gate), pass_by_pairs, grouped, e)
            if e > 0:
                hidden.append(quantise(keep, h, "_h%d" % (e - 1)))
            if e == LAST - 1:
                break
            w3_raw = load_passes(w3, e, 0, PASSES)
            banks, one_pass = (pair_banks, pass_by_pairs) if e < BY_RANKS else (rank_banks, pass_by_ranks)
            linear_sums = matrix_sums(banks(psum_linear), one_pass, round_matrix(w3_raw, copies), e)
            if e > 0:
                gates = sigmoids(gate_sums, w3_raw[:, 1])
            if e == LATE_W2 - 1:
                early_raw = load_w2(raw_pool, 0, LATE_W2, "raw", 4096)
                early_codes = round_w2(early_raw[:], LATE_W2, matrix_stage, matrix_code_pool, "matrix_grouped")
            if e == LATE_W2 + 1:
                result = w1_raw[:, 1, 0:R, :].rearrange("p m (e u) -> p m e u", u=U)
                for e0 in range(0, LATE_W2, 2):
                    results(e0, early_codes[e0 : e0 + 2], result[:, :, e0 : e0 + 2, :])
                stores.append((out_view[:, :, 0:LATE_W2, :], result))

        linear_sums = rank_banks(psum_linear)
        for o in range(PASSES):
            w3_raw = load_passes(w3, LAST - 1, o, 1)
            copies = scalar_alone if o == 0 else vector_then_scalar
            pass_by_ranks(linear_sums, pair_codes(round_pairs(w3_raw[:, 0], copies)), LAST - 1, o)
        gates = sigmoids(gate_sums, w3_raw[:, 0])

        rounded = round_pairs(load_passes(w1, LAST, 0, 1)[:, 0], vector_then_scalar)
        h = work.tile([P, C * PACK], BF16, name="h", align_bytes=64)
        products_by_ranks(h[:], linear_sums, gates)
        gate_sums = pair_banks(psum_gate)
        pass_by_pairs(gate_sums, pair_codes(rounded), LAST, 0)
        hidden.append(quantise(keep, h[:], "_h%d" % (LAST - 1)))
        second = pair_codes(round_pairs(load_passes(w1, LAST, 1, 1)[:, 0], vector_then_scalar))
        pass_by_pairs(gate_sums, second, LAST, 1)
        w3_raw = load_passes(w3, LAST, 0, 1)
        rounded = round_pairs(w3_raw[:, 0], vector_then_scalar)
        gates = sigmoids(gate_sums, w3_raw[:, 0])
        linear_sums = rank_banks(psum_linear)
        third = pair_codes(rounded)
        pass_by_ranks(linear_sums, third, LAST, 0)
        last_raw = load_passes(w3, LAST, 1, 1)
        late_raw = [load_w2(token_pool, e, 1, "w2_raw%d" % e, 2048) for e in range(LATE_W2, E)]
        pass_by_ranks(linear_sums, pair_codes(round_pairs(last_raw[:, 0], vector_alone)), LAST, 1)
        late_codes = [round_w2(raw[:], 1, stage, code_pool, "grouped")[0] for raw in late_raw]
        late_results(LATE_W2, late_codes[0:2])
        late_results(LATE_W2 + 2, late_codes[2:3])
        h_ranks = []
        for m in range(R):
            h = work.tile([P, U * PACK], BF16, name="h", align_bytes=64)
            product_of_rank(h[:], linear_sums[m], gates, m)
            h_ranks.append(h)
        for m, copy in enumerate([nc.scalar.copy, nc.vector.tensor_copy]):
            rank_codes = quantise(keep, h_ranks[m][:], "_rank%d" % m)
            bank = psum_y.tile([P, U], F32, name="y", tag="y")
            second_layer_matmul(bank[:], late_codes[-1], rank_codes)
            result = keep.tile([P, U], F32, name="rank_result%d" % m, align_bytes=256)
            copy(result[:], bank[:])
            stores.append((out_view[:, m, LAST, :], result[:]))

        for place, result in stores:
            nc.sync.dma_start(place, result)
